import numpy as np
import ml_dtypes


def mxq(x, axis, fmt="e4m3"):
    dtype, down = {"e4m3": (ml_dtypes.float8_e4m3fn, 7), "e5m2": (ml_dtypes.float8_e5m2, 14)}[fmt]
    v = np.moveaxis(np.asarray(x, np.float32).astype(ml_dtypes.bfloat16).astype(np.float64), axis, -1)
    blocks = v.reshape(v.shape[:-1] + (-1, 32))
    amax = np.abs(blocks).max(-1, keepdims=True)
    byte = np.maximum(np.where(amax > 0, np.frexp(amax)[1] - 1 + 127, 0) - down, 1)
    scale = np.exp2(byte - 127.0)
    codes = (blocks / scale).astype(np.float32).astype(dtype).astype(np.float64)
    return np.moveaxis((codes * scale).reshape(v.shape), -1, axis)


WIDE = False


def mx_kscale(k):
    if not WIDE:
        return np.ones(k)
    levels = np.array([10, -10, 5, -5, 0])
    if k % 512:
        return np.exp2(np.random.permutation(np.resize(levels, k // 32))).repeat(32)
    a = np.empty((k // 512, 16))
    for p in range(k // 512):
        a[p, :8] = np.random.permutation(np.resize(levels, 8))
        for g in range(8):
            far = levels[np.abs(levels - a[p, g]) >= 10]
            a[p, g + 8] = far[np.random.randint(len(far))]
    return np.exp2(a.ravel()).repeat(32)


def f64(x):
    return np.asarray(x).astype(np.float64)


def striped(idx):
    return np.tile(np.asarray(idx).reshape(-1, 16).T, (8, 1)).astype(np.uint16)


def unstriped(offs):
    return offs[:16].T.reshape(-1).astype(np.int64)


E2M1 = np.array([0.0, 0.5, 1.0, 1.5, 2.0, 3.0, 4.0, 6.0, -0.0, -0.5, -1.0, -1.5, -2.0, -3.0, -4.0, -6.0])


def pack_weight(w, fmt):
    k, n = w.shape
    w = f64(np.asarray(w, np.float32).astype(ml_dtypes.bfloat16)).reshape(k // 32, 32, n)
    amax = np.abs(w).max(1)
    if fmt == "e4m3":
        byte = np.frexp(amax)[1] - 1 + 127 - 7
    else:
        mant, ex = np.frexp(amax / 6.0)
        byte = np.where(mant > 0.5, ex, ex - 1) + 127
    byte = np.clip(np.where(amax > 0, byte, 1), 1, 254)
    scaled = (w * np.exp2(127.0 - byte)[:, None, :]).reshape(k, n).astype(np.float32)
    by_word = np.ascontiguousarray(scaled.reshape(k // 512, 128, 4, n).transpose(0, 1, 3, 2))
    if fmt == "e4m3":
        words = by_word.astype(ml_dtypes.float8_e4m3fn).view(np.uint8)
    else:
        c = by_word.astype(ml_dtypes.float4_e2m1fn).view(np.uint8) & 0xF
        words = (c[..., 0::2] | (c[..., 1::2] << 4)).reshape(k // 512, 128, 2 * n)
    return np.ascontiguousarray(words), np.ascontiguousarray(byte.astype(np.uint8).reshape(k // 512, 16, n))


def unpack_weight(words, scales, fmt):
    g, _, n = scales.shape
    words = np.ascontiguousarray(words).reshape(g, 128, n, -1)
    if fmt == "e4m3":
        vals = words.view(ml_dtypes.float8_e4m3fn).astype(np.float64)
    else:
        nib = np.empty((g, 128, n, 4), np.uint8)
        nib[..., 0::2] = words & 0xF
        nib[..., 1::2] = words >> 4
        vals = E2M1[nib]
    vals = vals * np.repeat(np.exp2(scales.astype(np.float64) - 127.0), 8, axis=1)[..., None]
    return vals.transpose(0, 1, 3, 2).reshape(g * 512, n)


B, N, T, D, NQ = 1, 512, 2048, 1024, 512
SEG = 16


def setup_inputs():
    n = np.random.standard_normal
    idx = np.random.permutation(T)[:B * N]
    s = mx_kscale(D)[:, None]
    kp = pack_weight(n((D, T)) / s, "e2m1")
    return {
        "qT": (n((B, D, NQ)) * s * (1.00 / np.sqrt(D))).astype(np.float32),
        "k_words": np.ascontiguousarray(kp[0].reshape(1, 2, 128, T, 2).transpose(0, 2, 3, 1, 4)).reshape(1, 128, T, 4),
        "k_scales": kp[1],
        "ls": (np.random.uniform(7.8, 8.4, (B, 1, NQ))).astype(np.float32),
        "dc": (np.random.uniform(0.1, 1.0, (B, 1, NQ))).astype(np.float32),
        "offs": striped(idx),
    }


def reference(qT, k_words, k_scales, ls, dc, offs):
    idx = unstriped(offs)
    pick = lambda x, which: x[:, which].reshape(x.shape[0], B, -1).transpose(1, 0, 2)
    k = unpack_weight(k_words.reshape(1, 128, T, 2, 2).transpose(0, 3, 1, 2, 4).reshape(2, 128, 2 * T), k_scales, "e2m1")
    kg = pick(k, idx)
    qq = mxq(f64(qT), 1, "e4m3")
    a = kg.transpose(0, 2, 1) @ qq
    y = (np.exp(a - f64(ls)) * f64(dc)).reshape(B, N, NQ // SEG, SEG).sum(-1)
    return y

@@ -1,0 +1,177 @@
+from contextlib import ExitStack
+
+import concourse.mybir as mybir
+from concourse.masks import make_identity
+
+F32 = mybir.dt.float32
+BF16 = mybir.dt.bfloat16
+I32 = mybir.dt.int32
+U32 = mybir.dt.uint32
+U16 = mybir.dt.uint16
+U8 = mybir.dt.uint8
+FP8X4 = mybir.dt.float8_e4m3fn_x4
+FP4X4 = mybir.dt.float4_e2m1fn_x4
+ACT = mybir.ActivationFunctionType
+ALU = mybir.AluOpType
+
+P = 128
+N, T, D, NQ = 512, 2048, 1024, 512
+SEG = 16
+PACK = 4
+PASSES = 2
+PAIR = 256
+FLOPS = 2 * N * D * NQ
+
+
+def tile_attend_tok_decayw_topk_kernel(tc, qT, k_words, k_scales, ls, dc, offs, out):
+    nc = tc.nc
+    with ExitStack() as ctx:
+        keep = ctx.enter_context(tc.tile_pool(name="keep", bufs=1))
+        psum = ctx.enter_context(tc.psum_pool(name="psum", bufs=1))
+
+        offsets = keep.tile([P, N // 16], U16, name="offsets")
+        nc.sync.dma_start(offsets[:], offs)
+
+        row_consts = keep.tile([2, NQ], F32, name="row_consts")
+        nc.sync.dma_start(row_consts[0:1, :], ls[0])
+        nc.sync.dma_start(row_consts[1:2, :], dc[0])
+
+        scale_rows = keep.tile([P, T], U8, name="scale_rows", align_bytes=64)
+        nc.gpsimd.memset(scale_rows[:].bitcast(I32), 0)
+        nc.scalar.dma_start(scale_rows[0:P:4, :].bitcast(I32), k_scales.rearrange("o f t -> f o t").bitcast(I32))
+
+        key_words = keep.tile([P, T], I32, name="key_words", align_bytes=64)
+        nc.sync.dma_start(key_words[:], k_words[0].rearrange("p t b -> p (t b)").bitcast(I32))
+
+        q_rows = qT[0].rearrange("(o p j) w -> o p j w", o=PASSES, j=PACK)
+        q_first = keep.tile([P, PACK, NQ], F32, name="q_first")
+        nc.sync.dma_start(q_first[:], q_rows[0])
+        q_second = []
+        for h in range(2):
+            part = keep.tile([P, PACK, PAIR], F32, name=f"q_second{h}")
+            nc.sync.dma_start(part[:], q_rows[1][:, :, h * PAIR : (h + 1) * PAIR])
+            q_second.append(part)
+
+        key_planes = keep.tile([P, PASSES, N], U8, name="key_planes", align_bytes=64)
+        nc.vector.memset(key_planes[:].rearrange("p o n -> p (o n)").bitcast(I32), 0)
+
+        ident = keep.tile([P, P], F32, name="ident")
+        make_identity(nc, ident[:])
+        dealt_consts = keep.tile([P, 2, 2, P], F32, name="dealt_consts")
+        nc.vector.memset(dealt_consts[:], 0.0)
+        nc.vector.tensor_copy(
+            dealt_consts[0:2].rearrange("p h m (g i) -> p h m g i", i=8),
+            row_consts[:].rearrange("p (h g m i) -> p h m g i", h=2, m=2, i=8),
+        )
+        turned = psum.tile([P, 4, P], F32, name="turned", tag="sum_a")
+        for c in range(4):
+            nc.tensor.transpose(turned[:, c, :], dealt_consts[:, c // 2, c % 2, :], ident[:])
+        neg_ls = keep.tile([P, 4], F32, name="neg_ls")
+        nc.scalar.activation(neg_ls[:], turned[:, :, 0], ACT.Copy, scale=-1.0)
+        decay = keep.tile([P, 4], F32, name="decay")
+        nc.scalar.copy(decay[:], turned[:, :, 1])
+
+        listed_scales = keep.tile([P, N], U8, name="listed_scales", align_bytes=64)
+        nc.vector.tensor_copy(listed_scales[:], scale_rows[:].indirect(offsets[:]))
+        for quad in range(4):
+            nc.scalar.dma_start(
+                key_planes[32 * quad : 32 * quad + 4].bitcast(I32),
+                listed_scales[32 * quad : 32 * quad + 32 : 4, :].bitcast(I32),
+            )
+
+        listed_words = keep.tile([P, N], U32, name="listed_words", align_bytes=64)
+        nc.vector.tensor_copy(listed_words[:], key_words[:].bitcast(U32).indirect(offsets[:]))
+        key_codes = []
+        for o in range(PASSES):
+            half = keep.tile([P, 2 * N], U8, name=f"key_codes{o}", align_bytes=64)
+            nc.vector.tensor_copy(
+                half[:].bitcast(U16), listed_words[:].bitcast(U16).rearrange("p (n o) -> p o n", o=PASSES)[:, o, :]
+            )
+            key_codes.append(half)
+
+        scores = [psum.tile([P, N], F32, name=f"scores{c}") for c in range(4)]
+
+        def cast(o, h, m, engine):
+            raw = q_first[:, :, h * PAIR : (h + 1) * PAIR] if o == 0 else q_second[h][:]
+            grouped = keep.tile([P, P, PACK], BF16, name=f"grouped{o}{h}{m}", align_bytes=64)
+            src = raw.rearrange("p j (g m c i) -> p m g c j i", m=2, c=2, i=4)[:, m]
+            dst = grouped[:].rearrange("p (g c i) j -> p g c j i", c=2, i=4)
+            if engine == "vector":
+                nc.vector.tensor_copy(dst, src)
+            else:
+                nc.scalar.copy(dst, src)
+            return grouped
+
+        def score(o, h, m, grouped):
+            codes = keep.tile([P, P], U32, name=f"q_codes{o}{h}{m}", align_bytes=64)
+            plane = keep.tile([P, P], U8, name=f"q_plane{o}{h}{m}", align_bytes=64)
+            nc.vector.quantize_mx(
+                out=codes[:].bitcast(FP8X4), scales=plane[:], in_=grouped[:].rearrange("p w j -> p (w j)")
+            )
+            nc.tensor.matmul_mx(
+                out=scores[2 * h + m][:],
+                lhsT=codes[:].bitcast(FP8X4),
+                lhsT_scale=plane[:],
+                rhs=key_codes[o][:].bitcast(FP4X4),
+                rhs_scale=key_planes[:, o, :],
+                start=(o == 0),
+                stop=(o == PASSES - 1),
+            )
+
+        def weigh(h, m, pieces):
+            raised = keep.tile([P, 4, P], F32, name=f"raised{h}{m}")
+            weights = keep.tile([P, 4, P], F32, name=f"weights{h}{m}")
+            dealt = scores[2 * h + m][:].rearrange("p (s r) -> p r s", r=4)
+            width = 4 // pieces
+            for u in range(pieces):
+                rs = slice(u * width, (u + 1) * width)
+                nc.scalar.activation(raised[:, rs, :], dealt[:, rs, :], ACT.Exp, bias=neg_ls[:, 2 * h + m : 2 * h + m + 1])
+                nc.vector.tensor_scalar(
+                    weights[:, rs, :], raised[:, rs, :], decay[:, 2 * h + m : 2 * h + m + 1], None, op0=ALU.mult
+                )
+            return weights
+
+        first = {(h, m): cast(0, h, m, "vector" if (h, m) == (0, 0) else "scalar") for h in range(2) for m in range(2)}
+        for m in range(2):
+            score(0, 0, m, first[0, m])
+        second = [cast(1, 0, m, "vector") for m in range(2)]
+        for m in range(2):
+            score(1, 0, m, second[m])
+        for m in range(2):
+            score(0, 1, m, first[1, m])
+        second = [cast(1, 1, m, "vector") for m in range(2)]
+        for m in range(2):
+            score(1, 1, m, second[m])
+
+        result = keep.tile([P, 4, NQ // SEG], F32, name="result")
+
+        weights_a = [weigh(0, m, 1) for m in range(2)]
+        sum_a = psum.tile([P, 4, P], F32, name="sum_a", tag="sum_a")
+        for r in range(4):
+            for m in range(2):
+                nc.tensor.matmul(
+                    sum_a[:, r, :], weights_a[m][:, r, :], ident[:], start=(m == 0), stop=(m == 1), is_transpose=True
+                )
+
+        weights_b = [weigh(1, 0, 1)]
+        nc.vector.tensor_reduce(
+            result[:, :, 0:16],
+            sum_a[:].rearrange("p r (g i) -> p r g i", i=8),
+            axis=mybir.AxisListType.X,
+            op=ALU.add,
+        )
+        weights_b.append(weigh(1, 1, 2))
+        sums_b = [psum.tile([P, P], F32, name=f"sum_b{r}", tag="scores0" if r == 3 else f"sum_b{r}") for r in range(4)]
+        for m in range(2):
+            for r in range(4):
+                nc.tensor.matmul(
+                    sums_b[r][:], weights_b[m][:, r, :], ident[:], start=(m == 0), stop=(m == 1), is_transpose=True
+                )
+        for r in range(4):
+            nc.vector.tensor_reduce(
+                result[:, r, 16:32],
+                sums_b[r][:].rearrange("p (g i) -> p g i", i=8),
+                axis=mybir.AxisListType.X,
+                op=ALU.add,
+            )
+        nc.sync.dma_start(out[0].rearrange("(s r) j -> s r j", r=4), result[:])

@@ -27,18 +27,20 @@ def tile_attend_tok_decayw_topk_kernel(tc, qT, k_words, k_scales, ls, dc, offs, 
     nc = tc.nc
     with ExitStack() as ctx:
         keep = ctx.enter_context(tc.tile_pool(name="keep", bufs=1))
+        shared = ctx.enter_context(tc.tile_pool(name="shared", bufs=1))
         psum = ctx.enter_context(tc.psum_pool(name="psum", bufs=1))
+
+        scale_rows = shared.tile([P, T], U8, name="scale_rows", offset=3072)
+        nc.sync.dma_start(scale_rows[0:32, :].bitcast(I32), k_scales.rearrange("o f t -> f o t").bitcast(I32))
+        nc.vector.memset(scale_rows[32:64, :].bitcast(I32), 0)
+        nc.vector.memset(scale_rows[64:P, :].bitcast(I32), 0)
 
         offsets = keep.tile([P, N // 16], U16, name="offsets")
         nc.sync.dma_start(offsets[:], offs)
 
         row_consts = keep.tile([2, NQ], F32, name="row_consts")
-        nc.sync.dma_start(row_consts[0:1, :], ls[0])
-        nc.sync.dma_start(row_consts[1:2, :], dc[0])
-
-        scale_rows = keep.tile([P, T], U8, name="scale_rows", align_bytes=64)
-        nc.gpsimd.memset(scale_rows[:].bitcast(I32), 0)
-        nc.scalar.dma_start(scale_rows[0:P:4, :].bitcast(I32), k_scales.rearrange("o f t -> f o t").bitcast(I32))
+        nc.scalar.dma_start(row_consts[0:1, :], ls[0])
+        nc.scalar.dma_start(row_consts[1:2, :], dc[0])
 
         key_words = keep.tile([P, T], I32, name="key_words", align_bytes=64)
         nc.sync.dma_start(key_words[:], k_words[0].rearrange("p t b -> p (t b)").bitcast(I32))
@@ -46,38 +48,38 @@ def tile_attend_tok_decayw_topk_kernel(tc, qT, k_words, k_scales, ls, dc, offs, 
         q_rows = qT[0].rearrange("(o p j) w -> o p j w", o=PASSES, j=PACK)
         q_first = keep.tile([P, PACK, NQ], F32, name="q_first")
         nc.sync.dma_start(q_first[:], q_rows[0])
-        q_second = []
-        for h in range(2):
-            part = keep.tile([P, PACK, PAIR], F32, name=f"q_second{h}")
-            nc.sync.dma_start(part[:], q_rows[1][:, :, h * PAIR : (h + 1) * PAIR])
-            q_second.append(part)
 
         key_planes = keep.tile([P, PASSES, N], U8, name="key_planes", align_bytes=64)
         nc.vector.memset(key_planes[:].rearrange("p o n -> p (o n)").bitcast(I32), 0)
 
         ident = keep.tile([P, P], F32, name="ident")
         make_identity(nc, ident[:])
+        listed_scales = keep.tile([P, N], U8, name="listed_scales", align_bytes=64)
+        nc.vector.tensor_copy(listed_scales[:], scale_rows[:].indirect(offsets[:]))
+        for quad in range(4):
+            nc.sync.dma_start(
+                key_planes[32 * quad : 32 * quad + 4].bitcast(I32),
+                listed_scales[8 * quad : 8 * quad + 8, :].bitcast(I32),
+            )
+        q_second = []
+        for h in range(2):
+            part = shared.tile([P, PACK, PAIR], F32, name=f"q_second{h}", offset=4096 * h)
+            nc.sync.dma_start(part[:], q_rows[1][:, :, h * PAIR : (h + 1) * PAIR])
+            q_second.append(part)
+
         dealt_consts = keep.tile([P, 2, 2, P], F32, name="dealt_consts")
         nc.vector.memset(dealt_consts[:], 0.0)
         nc.vector.tensor_copy(
-            dealt_consts[0:2].rearrange("p h m (g i) -> p h m g i", i=8),
-            row_consts[:].rearrange("p (h g m i) -> p h m g i", h=2, m=2, i=8),
+            dealt_consts[0:2].rearrange("p m h (g i) -> p m (h g) i", i=8),
+            row_consts[:].rearrange("p (g m i) -> p m g i", m=2, i=8),
         )
         turned = psum.tile([P, 4, P], F32, name="turned", tag="sum_a")
         for c in range(4):
-            nc.tensor.transpose(turned[:, c, :], dealt_consts[:, c // 2, c % 2, :], ident[:])
+            nc.tensor.transpose(turned[:, c, :], dealt_consts[:, c % 2, c // 2, :], ident[:])
         neg_ls = keep.tile([P, 4], F32, name="neg_ls")
         nc.scalar.activation(neg_ls[:], turned[:, :, 0], ACT.Copy, scale=-1.0)
         decay = keep.tile([P, 4], F32, name="decay")
         nc.scalar.copy(decay[:], turned[:, :, 1])
-
-        listed_scales = keep.tile([P, N], U8, name="listed_scales", align_bytes=64)
-        nc.vector.tensor_copy(listed_scales[:], scale_rows[:].indirect(offsets[:]))
-        for quad in range(4):
-            nc.scalar.dma_start(
-                key_planes[32 * quad : 32 * quad + 4].bitcast(I32),
-                listed_scales[32 * quad : 32 * quad + 32 : 4, :].bitcast(I32),
-            )
 
         listed_words = keep.tile([P, N], U32, name="listed_words", align_bytes=64)
         nc.vector.tensor_copy(listed_words[:], key_words[:].bitcast(U32).indirect(offsets[:]))
@@ -93,7 +95,10 @@ def tile_attend_tok_decayw_topk_kernel(tc, qT, k_words, k_scales, ls, dc, offs, 
 
         def cast(o, h, m, engine):
             raw = q_first[:, :, h * PAIR : (h + 1) * PAIR] if o == 0 else q_second[h][:]
-            grouped = keep.tile([P, P, PACK], BF16, name=f"grouped{o}{h}{m}", align_bytes=64)
+            if (o, h) == (0, 1):
+                grouped = shared.tile([P, P, PACK], BF16, name=f"grouped{o}{h}{m}", align_bytes=64, offset=1024 * m)
+            else:
+                grouped = keep.tile([P, P, PACK], BF16, name=f"grouped{o}{h}{m}", align_bytes=64)
             src = raw.rearrange("p j (g m c i) -> p m g c j i", m=2, c=2, i=4)[:, m]
             dst = grouped[:].rearrange("p (g c i) j -> p g c j i", c=2, i=4)
             if engine == "vector":
@@ -131,17 +136,13 @@ def tile_attend_tok_decayw_topk_kernel(tc, qT, k_words, k_scales, ls, dc, offs, 
                 )
             return weights
 
-        first = {(h, m): cast(0, h, m, "vector" if (h, m) == (0, 0) else "scalar") for h in range(2) for m in range(2)}
+        for o, engines in ((0, "vs"), (1, "vs")):
+            rounded = [cast(o, 0, m, "vector" if engines[m] == "v" else "scalar") for m in range(2)]
+            for m in range(2):
+                score(o, 0, m, rounded[m])
         for m in range(2):
-            score(0, 0, m, first[0, m])
-        second = [cast(1, 0, m, "vector") for m in range(2)]
-        for m in range(2):
-            score(1, 0, m, second[m])
-        for m in range(2):
-            score(0, 1, m, first[1, m])
-        second = [cast(1, 1, m, "vector") for m in range(2)]
-        for m in range(2):
-            score(1, 1, m, second[m])
+            for o in range(PASSES):
+                score(o, 1, m, cast(o, 1, m, "vector" if o else "scalar"))
 
         result = keep.tile([P, 4, NQ // SEG], F32, name="result")
 
@@ -160,7 +161,7 @@ def tile_attend_tok_decayw_topk_kernel(tc, qT, k_words, k_scales, ls, dc, offs, 
             axis=mybir.AxisListType.X,
             op=ALU.add,
         )
-        weights_b.append(weigh(1, 1, 2))
+        weights_b.append(weigh(1, 1, 4))
         sums_b = [psum.tile([P, P], F32, name=f"sum_b{r}", tag="scores0" if r == 3 else f"sum_b{r}") for r in range(4)]
         for m in range(2):
             for r in range(4):

@@ -95,8 +95,10 @@ def tile_attend_tok_decayw_topk_kernel(tc, qT, k_words, k_scales, ls, dc, offs, 
 
         def cast(o, h, m, engine):
             raw = q_first[:, :, h * PAIR : (h + 1) * PAIR] if o == 0 else q_second[h][:]
-            if (o, h) == (0, 1):
-                grouped = shared.tile([P, P, PACK], BF16, name=f"grouped{o}{h}{m}", align_bytes=64, offset=1024 * m)
+            if (o, h, m) == (1, 0, 1):
+                grouped = shared.tile([P, P, PACK], BF16, name="grouped101", align_bytes=64, offset=8192)
+            elif (o, h, m) == (0, 1, 1):
+                grouped = shared.tile([P, P, PACK], BF16, name="grouped011", align_bytes=64, offset=0)
             else:
                 grouped = keep.tile([P, P, PACK], BF16, name=f"grouped{o}{h}{m}", align_bytes=64)
             src = raw.rearrange("p j (g m c i) -> p m g c j i", m=2, c=2, i=4)[:, m]
@@ -108,7 +110,10 @@ def tile_attend_tok_decayw_topk_kernel(tc, qT, k_words, k_scales, ls, dc, offs, 
             return grouped
 
         def score(o, h, m, grouped):
-            codes = keep.tile([P, P], U32, name=f"q_codes{o}{h}{m}", align_bytes=64)
+            if (o, h, m) == (0, 1, 0):
+                codes = shared.tile([P, P], U32, name=f"q_codes{o}{h}{m}", align_bytes=64, offset=8192 + 512 * m)
+            else:
+                codes = keep.tile([P, P], U32, name=f"q_codes{o}{h}{m}", align_bytes=64)
             plane = keep.tile([P, P], U8, name=f"q_plane{o}{h}{m}", align_bytes=64)
             nc.vector.quantize_mx(
                 out=codes[:].bitcast(FP8X4), scales=plane[:], in_=grouped[:].rearrange("p w j -> p (w j)")
@@ -123,28 +128,37 @@ def tile_attend_tok_decayw_topk_kernel(tc, qT, k_words, k_scales, ls, dc, offs, 
                 stop=(o == PASSES - 1),
             )
 
+        raised_at = {}
+        weights_at = {0: 4096}
+
+        def placed(name, offset):
+            if offset is None:
+                return keep.tile([P, 4, P], F32, name=name)
+            return shared.tile([P, 4, P], F32, name=name, offset=offset)
+
         def weigh(h, m, pieces):
-            raised = keep.tile([P, 4, P], F32, name=f"raised{h}{m}")
-            weights = keep.tile([P, 4, P], F32, name=f"weights{h}{m}")
-            dealt = scores[2 * h + m][:].rearrange("p (s r) -> p r s", r=4)
+            c = 2 * h + m
+            raised = placed(f"raised{c}", raised_at.get(c))
+            weights = placed(f"weights{c}", weights_at.get(c))
+            dealt = scores[c][:].rearrange("p (s r) -> p r s", r=4)
             width = 4 // pieces
             for u in range(pieces):
                 rs = slice(u * width, (u + 1) * width)
-                nc.scalar.activation(raised[:, rs, :], dealt[:, rs, :], ACT.Exp, bias=neg_ls[:, 2 * h + m : 2 * h + m + 1])
-                nc.vector.tensor_scalar(
-                    weights[:, rs, :], raised[:, rs, :], decay[:, 2 * h + m : 2 * h + m + 1], None, op0=ALU.mult
-                )
+                nc.scalar.activation(raised[:, rs, :], dealt[:, rs, :], ACT.Exp, bias=neg_ls[:, c : c + 1])
+                nc.vector.tensor_scalar(weights[:, rs, :], raised[:, rs, :], decay[:, c : c + 1], None, op0=ALU.mult)
             return weights
 
-        for o, engines in ((0, "vs"), (1, "vs")):
-            rounded = [cast(o, 0, m, "vector" if engines[m] == "v" else "scalar") for m in range(2)]
-            for m in range(2):
-                score(o, 0, m, rounded[m])
+        rounded = [cast(0, 0, m, ("vector", "scalar")[m]) for m in range(2)]
         for m in range(2):
-            for o in range(PASSES):
-                score(o, 1, m, cast(o, 1, m, "vector" if o else "scalar"))
-
-        result = keep.tile([P, 4, NQ // SEG], F32, name="result")
+            score(0, 0, m, rounded[m])
+        early = [cast(0, 1, 0, "scalar")]
+        rounded = [cast(1, 0, m, ("vector", "scalar")[m]) for m in range(2)]
+        early.append(cast(0, 1, 1, "scalar"))
+        for m in range(2):
+            score(1, 0, m, rounded[m])
+        for m in range(2):
+            score(0, 1, m, early[m])
+            score(1, 1, m, cast(1, 1, m, "vector"))
 
         weights_a = [weigh(0, m, 1) for m in range(2)]
         sum_a = psum.tile([P, 4, P], F32, name="sum_a", tag="sum_a")
@@ -154,24 +168,34 @@ def tile_attend_tok_decayw_topk_kernel(tc, qT, k_words, k_scales, ls, dc, offs, 
                     sum_a[:, r, :], weights_a[m][:, r, :], ident[:], start=(m == 0), stop=(m == 1), is_transpose=True
                 )
 
-        weights_b = [weigh(1, 0, 1)]
+        weights_2 = weigh(1, 0, 1)
+        dealt = scores[3][:].rearrange("p (s r) -> p r s", r=4)
+        raised_3 = [
+            shared.tile([P, 2, P], F32, name="raised_3a", offset=10240),
+            keep.tile([P, 2, P], F32, name="raised_3b"),
+        ]
+        weights_3 = [keep.tile([P, 2, P], F32, name=f"weights_3{u}") for u in range(2)]
+        for u in range(2):
+            nc.scalar.activation(raised_3[u][:], dealt[:, 2 * u : 2 * u + 2, :], ACT.Exp, bias=neg_ls[:, 3:4])
+        nc.vector.tensor_scalar(weights_3[0][:], raised_3[0][:], decay[:, 3:4], None, op0=ALU.mult)
+        nc.scalar.activation(weights_3[1][:], raised_3[1][:], ACT.Copy, scale=decay[:, 3:4])
+        result = shared.tile([P, 4, NQ // SEG], F32, name="result", offset=10240)
         nc.vector.tensor_reduce(
             result[:, :, 0:16],
             sum_a[:].rearrange("p r (g i) -> p r g i", i=8),
             axis=mybir.AxisListType.X,
             op=ALU.add,
         )
-        weights_b.append(weigh(1, 1, 4))
-        sums_b = [psum.tile([P, P], F32, name=f"sum_b{r}", tag="scores0" if r == 3 else f"sum_b{r}") for r in range(4)]
-        for m in range(2):
-            for r in range(4):
+        for u in range(2):
+            sum_b = psum.tile([P, 2, P], F32, name=f"sum_b{u}")
+            for e in range(2):
                 nc.tensor.matmul(
-                    sums_b[r][:], weights_b[m][:, r, :], ident[:], start=(m == 0), stop=(m == 1), is_transpose=True
+                    sum_b[:, e, :], weights_2[:, 2 * u + e, :], ident[:], start=True, stop=False, is_transpose=True
                 )
-        for r in range(4):
+                nc.tensor.matmul(sum_b[:, e, :], weights_3[u][:, e, :], ident[:], start=False, stop=True, is_transpose=True)
             nc.vector.tensor_reduce(
-                result[:, r, 16:32],
-                sums_b[r][:].rearrange("p (g i) -> p g i", i=8),
+                result[:, 2 * u : 2 * u + 2, 16:32],
+                sum_b[:].rearrange("p r (g i) -> p r g i", i=8),
                 axis=mybir.AxisListType.X,
                 op=ALU.add,
             )

@@ -160,25 +160,34 @@ def tile_attend_tok_decayw_topk_kernel(tc, qT, k_words, k_scales, ls, dc, offs, 
             score(0, 1, m, early[m])
             score(1, 1, m, cast(1, 1, m, "vector"))
 
-        weights_a = [weigh(0, m, 1) for m in range(2)]
+        weights_0 = weigh(0, 0, 1)
+        raised_1 = keep.tile([P, 4, P], F32, name="raised1")
+        nc.scalar.activation(
+            raised_1[:], scores[1][:].rearrange("p (s r) -> p r s", r=4), ACT.Exp, bias=neg_ls[:, 1:2]
+        )
+        pair_a = keep.tile([P, 4, P], F32, name="pair_a")
+        nc.vector.scalar_tensor_tensor(
+            pair_a[:], raised_1[:], decay[:, 1:2], weights_0[:], op0=ALU.mult, op1=ALU.add
+        )
         sum_a = psum.tile([P, 4, P], F32, name="sum_a", tag="sum_a")
         for r in range(4):
-            for m in range(2):
-                nc.tensor.matmul(
-                    sum_a[:, r, :], weights_a[m][:, r, :], ident[:], start=(m == 0), stop=(m == 1), is_transpose=True
-                )
+            nc.tensor.transpose(sum_a[:, r, :], pair_a[:, r, :], ident[:])
 
         weights_2 = weigh(1, 0, 1)
         dealt = scores[3][:].rearrange("p (s r) -> p r s", r=4)
-        raised_3 = [
-            shared.tile([P, 2, P], F32, name="raised_3a", offset=10240),
-            keep.tile([P, 2, P], F32, name="raised_3b"),
-        ]
-        weights_3 = [keep.tile([P, 2, P], F32, name=f"weights_3{u}") for u in range(2)]
-        for u in range(2):
-            nc.scalar.activation(raised_3[u][:], dealt[:, 2 * u : 2 * u + 2, :], ACT.Exp, bias=neg_ls[:, 3:4])
-        nc.vector.tensor_scalar(weights_3[0][:], raised_3[0][:], decay[:, 3:4], None, op0=ALU.mult)
-        nc.scalar.activation(weights_3[1][:], raised_3[1][:], ACT.Copy, scale=decay[:, 3:4])
+        weights_3 = keep.tile([P, 2, P], F32, name="weights_3")
+        raised_a = shared.tile([P, 2, P], F32, name="raised_3a", offset=10240)
+        raised_b = keep.tile([P, P], F32, name="raised_3b")
+        weights_b = keep.tile([P, P], F32, name="weights_3b")
+        raised_c = keep.tile([P, P], F32, name="raised_3c")
+        weights_c = keep.tile([P, P], F32, name="weights_3c")
+        nc.scalar.activation(raised_a[:], dealt[:, 0:2, :], ACT.Exp, bias=neg_ls[:, 3:4])
+        nc.scalar.activation(raised_b[:], dealt[:, 2, :], ACT.Exp, bias=neg_ls[:, 3:4])
+        nc.scalar.activation(raised_c[:], dealt[:, 3, :], ACT.Exp, bias=neg_ls[:, 3:4])
+        nc.vector.tensor_scalar(weights_3[:], raised_a[:], decay[:, 3:4], None, op0=ALU.mult)
+        nc.scalar.activation(weights_b[:], raised_b[:], ACT.Copy, scale=decay[:, 3:4])
+        nc.scalar.activation(weights_c[:], raised_c[:], ACT.Copy, scale=decay[:, 3:4])
+        last = [weights_3[:, 0, :], weights_3[:, 1, :], weights_b[:], weights_c[:]]
         result = shared.tile([P, 4, NQ // SEG], F32, name="result", offset=10240)
         nc.vector.tensor_reduce(
             result[:, :, 0:16],
@@ -186,15 +195,13 @@ def tile_attend_tok_decayw_topk_kernel(tc, qT, k_words, k_scales, ls, dc, offs, 
             axis=mybir.AxisListType.X,
             op=ALU.add,
         )
-        for u in range(2):
-            sum_b = psum.tile([P, 2, P], F32, name=f"sum_b{u}")
-            for e in range(2):
-                nc.tensor.matmul(
-                    sum_b[:, e, :], weights_2[:, 2 * u + e, :], ident[:], start=True, stop=False, is_transpose=True
-                )
-                nc.tensor.matmul(sum_b[:, e, :], weights_3[u][:, e, :], ident[:], start=False, stop=True, is_transpose=True)
+        for rs in ((0, 1), (2,), (3,)):
+            sum_b = psum.tile([P, len(rs), P], F32, name=f"sum_b{rs[0]}")
+            for e, r in enumerate(rs):
+                nc.tensor.matmul(sum_b[:, e, :], weights_2[:, r, :], ident[:], start=True, stop=False, is_transpose=True)
+                nc.tensor.matmul(sum_b[:, e, :], last[r], ident[:], start=False, stop=True, is_transpose=True)
             nc.vector.tensor_reduce(
-                result[:, 2 * u : 2 * u + 2, 16:32],
+                result[:, rs[0] : rs[-1] + 1, 16:32],
                 sum_b[:].rearrange("p r (g i) -> p r g i", i=8),
                 axis=mybir.AxisListType.X,
                 op=ALU.add,

@@ -20,6 +20,7 @@ SEG = 16
 PACK = 4
 PASSES = 2
 PAIR = 256
+LEAD = 256
 FLOPS = 2 * N * D * NQ
 
 
@@ -30,6 +31,9 @@ def tile_attend_tok_decayw_topk_kernel(tc, qT, k_words, k_scales, ls, dc, offs, 
         shared = ctx.enter_context(tc.tile_pool(name="shared", bufs=1))
         psum = ctx.enter_context(tc.psum_pool(name="psum", bufs=1))
 
+        key_words = keep.tile([P, T], I32, name="key_words", align_bytes=64)
+        words_in = k_words[0].rearrange("p t b -> p (t b)").bitcast(I32)
+        nc.sync.dma_start(key_words[:, 0:LEAD], words_in[:, 0:LEAD])
         scale_rows = shared.tile([P, T], U8, name="scale_rows", offset=3072)
         nc.sync.dma_start(scale_rows[0:32, :].bitcast(I32), k_scales.rearrange("o f t -> f o t").bitcast(I32))
         nc.vector.memset(scale_rows[32:64, :].bitcast(I32), 0)
@@ -42,8 +46,7 @@ def tile_attend_tok_decayw_topk_kernel(tc, qT, k_words, k_scales, ls, dc, offs, 
         nc.scalar.dma_start(row_consts[0:1, :], ls[0])
         nc.scalar.dma_start(row_consts[1:2, :], dc[0])
 
-        key_words = keep.tile([P, T], I32, name="key_words", align_bytes=64)
-        nc.sync.dma_start(key_words[:], k_words[0].rearrange("p t b -> p (t b)").bitcast(I32))
+        nc.sync.dma_start(key_words[:, LEAD:T], words_in[:, LEAD:T])
 
         q_rows = qT[0].rearrange("(o p j) w -> o p j w", o=PASSES, j=PACK)
         q_first = keep.tile([P, PACK, NQ], F32, name="q_first")
@@ -162,13 +165,19 @@ def tile_attend_tok_decayw_topk_kernel(tc, qT, k_words, k_scales, ls, dc, offs, 
 
         weights_0 = weigh(0, 0, 1)
         raised_1 = keep.tile([P, 4, P], F32, name="raised1")
-        nc.scalar.activation(
-            raised_1[:], scores[1][:].rearrange("p (s r) -> p r s", r=4), ACT.Exp, bias=neg_ls[:, 1:2]
-        )
+        for u in range(2):
+            nc.scalar.activation(
+                raised_1[:, 2 * u : 2 * u + 2, :],
+                scores[1][:].rearrange("p (s r) -> p r s", r=4)[:, 2 * u : 2 * u + 2, :],
+                ACT.Exp,
+                bias=neg_ls[:, 1:2],
+            )
         pair_a = keep.tile([P, 4, P], F32, name="pair_a")
-        nc.vector.scalar_tensor_tensor(
-            pair_a[:], raised_1[:], decay[:, 1:2], weights_0[:], op0=ALU.mult, op1=ALU.add
-        )
+        for u in range(2):
+            rs = slice(2 * u, 2 * u + 2)
+            nc.vector.scalar_tensor_tensor(
+                pair_a[:, rs, :], raised_1[:, rs, :], decay[:, 1:2], weights_0[:, rs, :], op0=ALU.mult, op1=ALU.add
+            )
         sum_a = psum.tile([P, 4, P], F32, name="sum_a", tag="sum_a")
         for r in range(4):
             nc.tensor.transpose(sum_a[:, r, :], pair_a[:, r, :], ident[:])

@@ -19,8 +19,7 @@ N, T, D, NQ = 512, 2048, 1024, 512
 SEG = 16
 PACK = 4
 PASSES = 2
-PAIR = 256
-LEAD = 256
+HALF = 256
 FLOPS = 2 * N * D * NQ
 
 
@@ -31,13 +30,10 @@ def tile_attend_tok_decayw_topk_kernel(tc, qT, k_words, k_scales, ls, dc, offs, 
         shared = ctx.enter_context(tc.tile_pool(name="shared", bufs=1))
         psum = ctx.enter_context(tc.psum_pool(name="psum", bufs=1))
 
-        key_words = keep.tile([P, T], I32, name="key_words", align_bytes=64)
-        words_in = k_words[0].rearrange("p t b -> p (t b)").bitcast(I32)
-        nc.sync.dma_start(key_words[:, 0:LEAD], words_in[:, 0:LEAD])
-        scale_rows = shared.tile([P, T], U8, name="scale_rows", offset=3072)
-        nc.sync.dma_start(scale_rows[0:32, :].bitcast(I32), k_scales.rearrange("o f t -> f o t").bitcast(I32))
-        nc.vector.memset(scale_rows[32:64, :].bitcast(I32), 0)
-        nc.vector.memset(scale_rows[64:P, :].bitcast(I32), 0)
+        scale_rows = shared.tile([P, 3 * 4096], U8, name="scale_rows", offset=0)
+        nc.sync.dma_start(scale_rows[0:32, 0:T].bitcast(I32), k_scales.rearrange("o f t -> f o t").bitcast(I32))
+        nc.vector.memset(scale_rows[32:64, 0:T].bitcast(I32), 0)
+        nc.vector.memset(scale_rows[64:P, 0:T].bitcast(I32), 0)
 
         offsets = keep.tile([P, N // 16], U16, name="offsets")
         nc.sync.dma_start(offsets[:], offs)
@@ -46,11 +42,13 @@ def tile_attend_tok_decayw_topk_kernel(tc, qT, k_words, k_scales, ls, dc, offs, 
         nc.scalar.dma_start(row_consts[0:1, :], ls[0])
         nc.scalar.dma_start(row_consts[1:2, :], dc[0])
 
-        nc.sync.dma_start(key_words[:, LEAD:T], words_in[:, LEAD:T])
+        key_words = shared.tile([P, T], I32, name="key_words", align_bytes=64, offset=32768)
+        nc.sync.dma_start(key_words[:], k_words[0].rearrange("p t b -> p (t b)").bitcast(I32))
 
         q_rows = qT[0].rearrange("(o p j) w -> o p j w", o=PASSES, j=PACK)
-        q_first = keep.tile([P, PACK, NQ], F32, name="q_first")
-        nc.sync.dma_start(q_first[:], q_rows[0])
+        raw = {}
+        raw[0, 0] = keep.tile([P, PACK, HALF], F32, name="raw00")
+        nc.sync.dma_start(raw[0, 0][:], q_rows[0][:, :, 0:HALF])
 
         key_planes = keep.tile([P, PASSES, N], U8, name="key_planes", align_bytes=64)
         nc.vector.memset(key_planes[:].rearrange("p o n -> p (o n)").bitcast(I32), 0)
@@ -58,21 +56,21 @@ def tile_attend_tok_decayw_topk_kernel(tc, qT, k_words, k_scales, ls, dc, offs, 
         ident = keep.tile([P, P], F32, name="ident")
         make_identity(nc, ident[:])
         listed_scales = keep.tile([P, N], U8, name="listed_scales", align_bytes=64)
-        nc.vector.tensor_copy(listed_scales[:], scale_rows[:].indirect(offsets[:]))
+        nc.vector.tensor_copy(listed_scales[:], scale_rows[:, 0:T].indirect(offsets[:]))
         for quad in range(4):
             nc.sync.dma_start(
                 key_planes[32 * quad : 32 * quad + 4].bitcast(I32),
                 listed_scales[8 * quad : 8 * quad + 8, :].bitcast(I32),
             )
-        q_second = []
-        for h in range(2):
-            part = shared.tile([P, PACK, PAIR], F32, name=f"q_second{h}", offset=4096 * h)
-            nc.sync.dma_start(part[:], q_rows[1][:, :, h * PAIR : (h + 1) * PAIR])
-            q_second.append(part)
+        for slot, (h, o) in ((2, (0, 1)), (0, (1, 0)), (1, (1, 1))):
+            raw[h, o] = shared.tile([P, PACK, HALF], F32, name=f"raw{h}{o}", offset=4096 * slot)
+            nc.sync.dma_start(raw[h, o][:], q_rows[o][:, :, h * HALF : (h + 1) * HALF])
 
         dealt_consts = keep.tile([P, 2, 2, P], F32, name="dealt_consts")
-        nc.vector.memset(dealt_consts[:], 0.0)
-        nc.vector.tensor_copy(
+        zero_column = keep.tile([P, 1], F32, name="zero_column")
+        nc.vector.memset(zero_column[:], 0.0)
+        nc.scalar.copy(dealt_consts[:].rearrange("p m h w -> p (m h w)"), zero_column[:].to_broadcast([P, NQ]))
+        nc.scalar.copy(
             dealt_consts[0:2].rearrange("p m h (g i) -> p m (h g) i", i=8),
             row_consts[:].rearrange("p (g m i) -> p m g i", m=2, i=8),
         )
@@ -87,7 +85,8 @@ def tile_attend_tok_decayw_topk_kernel(tc, qT, k_words, k_scales, ls, dc, offs, 
         listed_words = keep.tile([P, N], U32, name="listed_words", align_bytes=64)
         nc.vector.tensor_copy(listed_words[:], key_words[:].bitcast(U32).indirect(offsets[:]))
         key_codes = []
-        for o in range(PASSES):
+
+        def split(o):
             half = keep.tile([P, 2 * N], U8, name=f"key_codes{o}", align_bytes=64)
             nc.vector.tensor_copy(
                 half[:].bitcast(U16), listed_words[:].bitcast(U16).rearrange("p (n o) -> p o n", o=PASSES)[:, o, :]
@@ -96,28 +95,30 @@ def tile_attend_tok_decayw_topk_kernel(tc, qT, k_words, k_scales, ls, dc, offs, 
 
         scores = [psum.tile([P, N], F32, name=f"scores{c}") for c in range(4)]
 
-        def cast(o, h, m, engine):
-            raw = q_first[:, :, h * PAIR : (h + 1) * PAIR] if o == 0 else q_second[h][:]
-            if (o, h, m) == (1, 0, 1):
-                grouped = shared.tile([P, P, PACK], BF16, name="grouped101", align_bytes=64, offset=8192)
-            elif (o, h, m) == (0, 1, 1):
-                grouped = shared.tile([P, P, PACK], BF16, name="grouped011", align_bytes=64, offset=0)
+        made = {}
+        grouped_at = {(0, 1, 0): 33792, (1, 1, 0): 20480}
+
+        def cast(h, o, m, engine):
+            if (h, o, m) in grouped_at:
+                grouped = shared.tile([P, P, PACK], BF16, name=f"grouped{h}{o}{m}", align_bytes=64, offset=grouped_at[h, o, m])
             else:
-                grouped = keep.tile([P, P, PACK], BF16, name=f"grouped{o}{h}{m}", align_bytes=64)
-            src = raw.rearrange("p j (g m c i) -> p m g c j i", m=2, c=2, i=4)[:, m]
+                grouped = keep.tile([P, P, PACK], BF16, name=f"grouped{h}{o}{m}", align_bytes=64)
+            src = raw[h, o][:].rearrange("p j (g m c i) -> p m g c j i", m=2, c=2, i=4)[:, m]
             dst = grouped[:].rearrange("p (g c i) j -> p g c j i", c=2, i=4)
             if engine == "vector":
                 nc.vector.tensor_copy(dst, src)
             else:
                 nc.scalar.copy(dst, src)
+            made[h, o, m, "cast"] = grouped
             return grouped
 
-        def score(o, h, m, grouped):
-            if (o, h, m) == (0, 1, 0):
-                codes = shared.tile([P, P], U32, name=f"q_codes{o}{h}{m}", align_bytes=64, offset=8192 + 512 * m)
+        def score(h, o, m, grouped):
+            if (h, o) == (0, 0):
+                codes = shared.tile([P, P], U32, name=f"q_codes{h}{o}{m}", align_bytes=64, offset=32768 + 512 * m)
             else:
-                codes = keep.tile([P, P], U32, name=f"q_codes{o}{h}{m}", align_bytes=64)
-            plane = keep.tile([P, P], U8, name=f"q_plane{o}{h}{m}", align_bytes=64)
+                codes = keep.tile([P, P], U32, name=f"q_codes{h}{o}{m}", align_bytes=64)
+            plane = keep.tile([P, P], U8, name=f"q_plane{h}{o}{m}", align_bytes=64)
+            made[h, o, m, "codes"] = codes
             nc.vector.quantize_mx(
                 out=codes[:].bitcast(FP8X4), scales=plane[:], in_=grouped[:].rearrange("p w j -> p (w j)")
             )
@@ -131,86 +132,61 @@ def tile_attend_tok_decayw_topk_kernel(tc, qT, k_words, k_scales, ls, dc, offs, 
                 stop=(o == PASSES - 1),
             )
 
-        raised_at = {}
-        weights_at = {0: 4096}
+        engines = {(0, 0): ("scalar", "scalar"), (0, 1): ("vector", "scalar"), (1, 0): ("vector", "scalar"), (1, 1): ("vector", "vector")}
+        for h in range(2):
+            for o in range(PASSES):
+                if h == 0:
+                    split(o)
+                rounded = [cast(h, o, m, engines[h, o][m]) for m in range(2)]
+                for m in range(2):
+                    score(h, o, m, rounded[m])
 
-        def placed(name, offset):
-            if offset is None:
-                return keep.tile([P, 4, P], F32, name=name)
-            return shared.tile([P, 4, P], F32, name=name, offset=offset)
+        def dealt(c):
+            return scores[c][:].rearrange("p (s r) -> p r s", r=4)
 
-        def weigh(h, m, pieces):
-            c = 2 * h + m
-            raised = placed(f"raised{c}", raised_at.get(c))
-            weights = placed(f"weights{c}", weights_at.get(c))
-            dealt = scores[c][:].rearrange("p (s r) -> p r s", r=4)
-            width = 4 // pieces
-            for u in range(pieces):
-                rs = slice(u * width, (u + 1) * width)
-                nc.scalar.activation(raised[:, rs, :], dealt[:, rs, :], ACT.Exp, bias=neg_ls[:, c : c + 1])
-                nc.vector.tensor_scalar(weights[:, rs, :], raised[:, rs, :], decay[:, c : c + 1], None, op0=ALU.mult)
-            return weights
-
-        rounded = [cast(0, 0, m, ("vector", "scalar")[m]) for m in range(2)]
-        for m in range(2):
-            score(0, 0, m, rounded[m])
-        early = [cast(0, 1, 0, "scalar")]
-        rounded = [cast(1, 0, m, ("vector", "scalar")[m]) for m in range(2)]
-        early.append(cast(0, 1, 1, "scalar"))
-        for m in range(2):
-            score(1, 0, m, rounded[m])
-        for m in range(2):
-            score(0, 1, m, early[m])
-            score(1, 1, m, cast(1, 1, m, "vector"))
-
-        weights_0 = weigh(0, 0, 1)
-        raised_1 = keep.tile([P, 4, P], F32, name="raised1")
-        for u in range(2):
-            nc.scalar.activation(
-                raised_1[:, 2 * u : 2 * u + 2, :],
-                scores[1][:].rearrange("p (s r) -> p r s", r=4)[:, 2 * u : 2 * u + 2, :],
-                ACT.Exp,
-                bias=neg_ls[:, 1:2],
-            )
-        pair_a = keep.tile([P, 4, P], F32, name="pair_a")
-        for u in range(2):
-            rs = slice(2 * u, 2 * u + 2)
-            nc.vector.scalar_tensor_tensor(
-                pair_a[:, rs, :], raised_1[:, rs, :], decay[:, 1:2], weights_0[:, rs, :], op0=ALU.mult, op1=ALU.add
-            )
+        result = keep.tile([P, 4, NQ // SEG], F32, name="result")
+        raised = [shared.tile([P, 4, P], F32, name=f"raised{c}", offset=(0, 2048, 30720)[c]) for c in range(3)]
+        weights = [shared.tile([P, 4, P], F32, name=f"weights{c}", offset=(18944, 24576, 26624)[c]) for c in range(3)]
+        for c in range(2):
+            nc.scalar.activation(raised[c][:], dealt(c), ACT.Exp, bias=neg_ls[:, c : c + 1])
+        nc.vector.tensor_scalar(weights[0][:], raised[0][:], decay[:, 0:1], None, op0=ALU.mult)
+        nc.vector.scalar_tensor_tensor(weights[1][:], raised[1][:], decay[:, 1:2], weights[0][:], op0=ALU.mult, op1=ALU.add)
         sum_a = psum.tile([P, 4, P], F32, name="sum_a", tag="sum_a")
         for r in range(4):
-            nc.tensor.transpose(sum_a[:, r, :], pair_a[:, r, :], ident[:])
+            nc.tensor.transpose(sum_a[:, r, :], weights[1][:, r, :], ident[:])
 
-        weights_2 = weigh(1, 0, 1)
-        dealt = scores[3][:].rearrange("p (s r) -> p r s", r=4)
-        weights_3 = keep.tile([P, 2, P], F32, name="weights_3")
-        raised_a = shared.tile([P, 2, P], F32, name="raised_3a", offset=10240)
-        raised_b = keep.tile([P, P], F32, name="raised_3b")
-        weights_b = keep.tile([P, P], F32, name="weights_3b")
-        raised_c = keep.tile([P, P], F32, name="raised_3c")
-        weights_c = keep.tile([P, P], F32, name="weights_3c")
-        nc.scalar.activation(raised_a[:], dealt[:, 0:2, :], ACT.Exp, bias=neg_ls[:, 3:4])
-        nc.scalar.activation(raised_b[:], dealt[:, 2, :], ACT.Exp, bias=neg_ls[:, 3:4])
-        nc.scalar.activation(raised_c[:], dealt[:, 3, :], ACT.Exp, bias=neg_ls[:, 3:4])
-        nc.vector.tensor_scalar(weights_3[:], raised_a[:], decay[:, 3:4], None, op0=ALU.mult)
-        nc.scalar.activation(weights_b[:], raised_b[:], ACT.Copy, scale=decay[:, 3:4])
-        nc.scalar.activation(weights_c[:], raised_c[:], ACT.Copy, scale=decay[:, 3:4])
-        last = [weights_3[:, 0, :], weights_3[:, 1, :], weights_b[:], weights_c[:]]
-        result = shared.tile([P, 4, NQ // SEG], F32, name="result", offset=10240)
+        nc.scalar.activation(raised[2][:], dealt(2), ACT.Exp, bias=neg_ls[:, 2:3])
+        nc.vector.tensor_scalar(weights[2][:], raised[2][:], decay[:, 2:3], None, op0=ALU.mult)
+        pieces = ((0, 2), (2, 3), (3, 4))
+        last_raised = []
+        for a, b in pieces:
+            piece = keep.tile([P, b - a, P], F32, name=f"raised3_{a}")
+            nc.scalar.activation(piece[:], dealt(3)[:, a:b, :], ACT.Exp, bias=neg_ls[:, 3:4])
+            last_raised.append(piece)
+        last_weights = []
+        for u, (a, b) in enumerate(pieces):
+            piece = keep.tile([P, b - a, P], F32, name=f"weights3_{a}")
+            if u == 0:
+                nc.vector.tensor_scalar(piece[:], last_raised[u][:], decay[:, 3:4], None, op0=ALU.mult)
+            else:
+                nc.scalar.activation(piece[:], last_raised[u][:], ACT.Copy, scale=decay[:, 3:4])
+            last_weights.append(piece)
         nc.vector.tensor_reduce(
             result[:, :, 0:16],
             sum_a[:].rearrange("p r (g i) -> p r g i", i=8),
             axis=mybir.AxisListType.X,
             op=ALU.add,
         )
-        for rs in ((0, 1), (2,), (3,)):
-            sum_b = psum.tile([P, len(rs), P], F32, name=f"sum_b{rs[0]}")
-            for e, r in enumerate(rs):
-                nc.tensor.matmul(sum_b[:, e, :], weights_2[:, r, :], ident[:], start=True, stop=False, is_transpose=True)
-                nc.tensor.matmul(sum_b[:, e, :], last[r], ident[:], start=False, stop=True, is_transpose=True)
+        sums_b = [psum.tile([P, b - a, P], F32, name=f"sum_b{a}") for a, b in pieces]
+        for u, (a, b) in enumerate(pieces):
+            for r in range(a, b):
+                nc.tensor.matmul(sums_b[u][:, r - a, :], weights[2][:, r, :], ident[:], start=(r == a), stop=False, is_transpose=True)
+        for u, (a, b) in enumerate(pieces):
+            sum_b = sums_b[u]
+            for r in range(a, b):
+                nc.tensor.matmul(sum_b[:, r - a, :], last_weights[u][:, r - a, :], ident[:], start=False, stop=(r == b - 1), is_transpose=True)
             nc.vector.tensor_reduce(
-                result[:, rs[0] : rs[-1] + 1, 16:32],
+                result[:, a:b, 16:32],
                 sum_b[:].rearrange("p r (g i) -> p r g i", i=8),
                 axis=mybir.AxisListType.X,
                 op=ALU.add,

@@ -30,10 +30,14 @@ def tile_attend_tok_decayw_topk_kernel(tc, qT, k_words, k_scales, ls, dc, offs, 
         shared = ctx.enter_context(tc.tile_pool(name="shared", bufs=1))
         psum = ctx.enter_context(tc.psum_pool(name="psum", bufs=1))
 
-        scale_rows = shared.tile([P, 3 * 4096], U8, name="scale_rows", offset=0)
-        nc.sync.dma_start(scale_rows[0:32, 0:T].bitcast(I32), k_scales.rearrange("o f t -> f o t").bitcast(I32))
-        nc.vector.memset(scale_rows[32:64, 0:T].bitcast(I32), 0)
-        nc.vector.memset(scale_rows[64:P, 0:T].bitcast(I32), 0)
+        q_rows = qT[0].rearrange("(o p j) w -> o p j w", o=PASSES, j=PACK)
+        early = keep.tile([P, PACK, HALF], F32, name="early")
+        nc.sync.dma_start(early[:, 0:1, :], q_rows[1][:, 0:1, 0:HALF])
+
+        scale_rows = keep.tile([P, T], U8, name="scale_rows")
+        nc.sync.dma_start(scale_rows[0:32, :].bitcast(I32), k_scales.rearrange("o f t -> f o t").bitcast(I32))
+        nc.vector.memset(scale_rows[32:64, :].bitcast(I32), 0)
+        nc.vector.memset(scale_rows[64:P, :].bitcast(I32), 0)
 
         offsets = keep.tile([P, N // 16], U16, name="offsets")
         nc.sync.dma_start(offsets[:], offs)
@@ -42,13 +46,11 @@ def tile_attend_tok_decayw_topk_kernel(tc, qT, k_words, k_scales, ls, dc, offs, 
         nc.scalar.dma_start(row_consts[0:1, :], ls[0])
         nc.scalar.dma_start(row_consts[1:2, :], dc[0])
 
+        nc.sync.dma_start(early[:, 1:PACK, :], q_rows[1][:, 1:PACK, 0:HALF])
         key_words = shared.tile([P, T], I32, name="key_words", align_bytes=64, offset=32768)
         nc.sync.dma_start(key_words[:], k_words[0].rearrange("p t b -> p (t b)").bitcast(I32))
-
-        q_rows = qT[0].rearrange("(o p j) w -> o p j w", o=PASSES, j=PACK)
-        raw = {}
-        raw[0, 0] = keep.tile([P, PACK, HALF], F32, name="raw00")
-        nc.sync.dma_start(raw[0, 0][:], q_rows[0][:, :, 0:HALF])
+        whole = shared.tile([P, PACK, NQ], F32, name="whole", offset=0)
+        nc.sync.dma_start(whole[:, 0:2, :], q_rows[0][:, 0:2, :])
 
         key_planes = keep.tile([P, PASSES, N], U8, name="key_planes", align_bytes=64)
         nc.vector.memset(key_planes[:].rearrange("p o n -> p (o n)").bitcast(I32), 0)
@@ -56,15 +58,16 @@ def tile_attend_tok_decayw_topk_kernel(tc, qT, k_words, k_scales, ls, dc, offs, 
         ident = keep.tile([P, P], F32, name="ident")
         make_identity(nc, ident[:])
         listed_scales = keep.tile([P, N], U8, name="listed_scales", align_bytes=64)
-        nc.vector.tensor_copy(listed_scales[:], scale_rows[:, 0:T].indirect(offsets[:]))
+        nc.vector.tensor_copy(listed_scales[:], scale_rows[:].indirect(offsets[:]))
         for quad in range(4):
             nc.sync.dma_start(
                 key_planes[32 * quad : 32 * quad + 4].bitcast(I32),
                 listed_scales[8 * quad : 8 * quad + 8, :].bitcast(I32),
             )
-        for slot, (h, o) in ((2, (0, 1)), (0, (1, 0)), (1, (1, 1))):
-            raw[h, o] = shared.tile([P, PACK, HALF], F32, name=f"raw{h}{o}", offset=4096 * slot)
-            nc.sync.dma_start(raw[h, o][:], q_rows[o][:, :, h * HALF : (h + 1) * HALF])
+        nc.sync.dma_start(whole[:, 2:PACK, :], q_rows[0][:, 2:PACK, :])
+        late = shared.tile([P, PACK, HALF], F32, name="late", offset=8192)
+        nc.sync.dma_start(late[:], q_rows[1][:, :, HALF:NQ])
+        raw = {(0, 0): whole[:, :, 0:HALF], (1, 0): whole[:, :, HALF:NQ], (0, 1): early[:], (1, 1): late[:]}
 
         dealt_consts = keep.tile([P, 2, 2, P], F32, name="dealt_consts")
         zero_column = keep.tile([P, 1], F32, name="zero_column")
@@ -77,33 +80,33 @@ def tile_attend_tok_decayw_topk_kernel(tc, qT, k_words, k_scales, ls, dc, offs, 
         turned = psum.tile([P, 4, P], F32, name="turned", tag="sum_a")
         for c in range(4):
             nc.tensor.transpose(turned[:, c, :], dealt_consts[:, c % 2, c // 2, :], ident[:])
-        neg_ls = keep.tile([P, 4], F32, name="neg_ls")
+        neg_ls = shared.tile([P, 4], F32, name="neg_ls", offset=16384)
         nc.scalar.activation(neg_ls[:], turned[:, :, 0], ACT.Copy, scale=-1.0)
         decay = keep.tile([P, 4], F32, name="decay")
         nc.scalar.copy(decay[:], turned[:, :, 1])
 
         listed_words = keep.tile([P, N], U32, name="listed_words", align_bytes=64)
         nc.vector.tensor_copy(listed_words[:], key_words[:].bitcast(U32).indirect(offsets[:]))
-        key_codes = []
+        key_codes = {}
 
         def split(o):
             half = keep.tile([P, 2 * N], U8, name=f"key_codes{o}", align_bytes=64)
             nc.vector.tensor_copy(
                 half[:].bitcast(U16), listed_words[:].bitcast(U16).rearrange("p (n o) -> p o n", o=PASSES)[:, o, :]
             )
-            key_codes.append(half)
+            key_codes[o] = half
 
         scores = [psum.tile([P, N], F32, name=f"scores{c}") for c in range(4)]
 
         made = {}
-        grouped_at = {(0, 1, 0): 33792, (1, 1, 0): 20480}
+        grouped_at = {(1, 1, 0): 20480}
 
         def cast(h, o, m, engine):
             if (h, o, m) in grouped_at:
                 grouped = shared.tile([P, P, PACK], BF16, name=f"grouped{h}{o}{m}", align_bytes=64, offset=grouped_at[h, o, m])
             else:
                 grouped = keep.tile([P, P, PACK], BF16, name=f"grouped{h}{o}{m}", align_bytes=64)
-            src = raw[h, o][:].rearrange("p j (g m c i) -> p m g c j i", m=2, c=2, i=4)[:, m]
+            src = raw[h, o].rearrange("p j (g m c i) -> p m g c j i", m=2, c=2, i=4)[:, m]
             dst = grouped[:].rearrange("p (g c i) j -> p g c j i", c=2, i=4)
             if engine == "vector":
                 nc.vector.tensor_copy(dst, src)
@@ -112,9 +115,9 @@ def tile_attend_tok_decayw_topk_kernel(tc, qT, k_words, k_scales, ls, dc, offs, 
             made[h, o, m, "cast"] = grouped
             return grouped
 
-        def score(h, o, m, grouped):
-            if (h, o) == (0, 0):
-                codes = shared.tile([P, P], U32, name=f"q_codes{h}{o}{m}", align_bytes=64, offset=32768 + 512 * m)
+        def quantise(h, o, m, grouped):
+            if (h, o, m) == (1, 0, 1):
+                codes = shared.tile([P, P], U32, name=f"q_codes{h}{o}{m}", align_bytes=64, offset=8192)
             else:
                 codes = keep.tile([P, P], U32, name=f"q_codes{h}{o}{m}", align_bytes=64)
             plane = keep.tile([P, P], U8, name=f"q_plane{h}{o}{m}", align_bytes=64)
@@ -122,73 +125,97 @@ def tile_attend_tok_decayw_topk_kernel(tc, qT, k_words, k_scales, ls, dc, offs, 
             nc.vector.quantize_mx(
                 out=codes[:].bitcast(FP8X4), scales=plane[:], in_=grouped[:].rearrange("p w j -> p (w j)")
             )
+            made[h, o, m, "plane"] = plane
+
+        def score(h, o, m, grouped):
+            if (h, o, m, "plane") not in made:
+                quantise(h, o, m, grouped)
+            codes, plane = made[h, o, m, "codes"], made[h, o, m, "plane"]
             nc.tensor.matmul_mx(
                 out=scores[2 * h + m][:],
                 lhsT=codes[:].bitcast(FP8X4),
                 lhsT_scale=plane[:],
                 rhs=key_codes[o][:].bitcast(FP4X4),
                 rhs_scale=key_planes[:, o, :],
-                start=(o == 0),
-                stop=(o == PASSES - 1),
+                start=(o == first_pass[h]),
+                stop=(o != first_pass[h]),
             )
 
-        engines = {(0, 0): ("scalar", "scalar"), (0, 1): ("vector", "scalar"), (1, 0): ("vector", "scalar"), (1, 1): ("vector", "vector")}
-        for h in range(2):
-            for o in range(PASSES):
-                if h == 0:
-                    split(o)
-                rounded = [cast(h, o, m, engines[h, o][m]) for m in range(2)]
-                for m in range(2):
-                    score(h, o, m, rounded[m])
+        first_pass = (1, 0)
+        split(1)
+        rounded = [cast(0, 1, m, ("vector", "scalar")[m]) for m in range(2)]
+        for m in range(2):
+            quantise(0, 1, m, rounded[m])
+        unread = psum.tile([P, N], F32, name="unread", tag="sum_b0")
+        for m in range(2):
+            nc.tensor.matmul_mx(
+                out=unread[:],
+                lhsT=made[0, 1, m, "codes"][:].bitcast(FP8X4),
+                lhsT_scale=made[0, 1, m, "plane"][:],
+                rhs=key_words[:, 0:HALF].bitcast(U8).bitcast(FP4X4),
+                rhs_scale=listed_scales[:],
+                start=True,
+                stop=True,
+            )
+        for m in range(2):
+            score(0, 1, m, rounded[m])
+        split(0)
+        rounded = [cast(h, 0, m, ("vector", "scalar")[m]) for h in range(2) for m in range(2)]
+        for c in range(3):
+            score(c // 2, 0, c % 2, rounded[c])
+        last = [cast(1, 1, m, "vector") for m in range(2)]
+        score(1, 1, 0, last[0])
+        score(1, 0, 1, rounded[3])
+        score(1, 1, 1, last[1])
 
         def dealt(c):
             return scores[c][:].rearrange("p (s r) -> p r s", r=4)
 
-        result = keep.tile([P, 4, NQ // SEG], F32, name="result")
+        results = [shared.tile([P, 2, NQ // SEG], F32, name=f"result{u}", offset=(16896, 16384)[u]) for u in range(2)]
         raised = [shared.tile([P, 4, P], F32, name=f"raised{c}", offset=(0, 2048, 30720)[c]) for c in range(3)]
         weights = [shared.tile([P, 4, P], F32, name=f"weights{c}", offset=(18944, 24576, 26624)[c]) for c in range(3)]
         for c in range(2):
             nc.scalar.activation(raised[c][:], dealt(c), ACT.Exp, bias=neg_ls[:, c : c + 1])
         nc.vector.tensor_scalar(weights[0][:], raised[0][:], decay[:, 0:1], None, op0=ALU.mult)
-        nc.vector.scalar_tensor_tensor(weights[1][:], raised[1][:], decay[:, 1:2], weights[0][:], op0=ALU.mult, op1=ALU.add)
-        sum_a = psum.tile([P, 4, P], F32, name="sum_a", tag="sum_a")
-        for r in range(4):
-            nc.tensor.transpose(sum_a[:, r, :], weights[1][:, r, :], ident[:])
+        halves = (slice(0, 2), slice(2, 4))
+        sums_a = [psum.tile([P, 2, P], F32, name=f"sum_a{u}", tag=("sum_a", "sum_a1")[u]) for u in range(2)]
+        for u, rs in enumerate(halves):
+            nc.vector.scalar_tensor_tensor(
+                weights[1][:, rs, :], raised[1][:, rs, :], decay[:, 1:2], weights[0][:, rs, :], op0=ALU.mult, op1=ALU.add
+            )
+            for e in range(2):
+                nc.tensor.transpose(sums_a[u][:, e, :], weights[1][:, 2 * u + e, :], ident[:])
+
+        def add_up(sums, u, h):
+            nc.vector.tensor_reduce(
+                results[u][:, :, 16 * h : 16 * h + 16],
+                sums[:].rearrange("p r (g i) -> p r g i", i=8),
+                axis=mybir.AxisListType.X,
+                op=ALU.add,
+            )
 
         nc.scalar.activation(raised[2][:], dealt(2), ACT.Exp, bias=neg_ls[:, 2:3])
         nc.vector.tensor_scalar(weights[2][:], raised[2][:], decay[:, 2:3], None, op0=ALU.mult)
+        sums_b = [psum.tile([P, 2, P], F32, name=f"sum_b{a}", tag=f"sum_b{a}") for a in (0, 2)]
+        for r in range(4):
+            nc.tensor.matmul(sums_b[r // 2][:, r % 2, :], weights[2][:, r, :], ident[:], start=(r % 2 == 0), stop=False, is_transpose=True)
         pieces = ((0, 2), (2, 3), (3, 4))
         last_raised = []
         for a, b in pieces:
             piece = keep.tile([P, b - a, P], F32, name=f"raised3_{a}")
             nc.scalar.activation(piece[:], dealt(3)[:, a:b, :], ACT.Exp, bias=neg_ls[:, 3:4])
             last_raised.append(piece)
-        last_weights = []
-        for u, (a, b) in enumerate(pieces):
-            piece = keep.tile([P, b - a, P], F32, name=f"weights3_{a}")
-            if u == 0:
-                nc.vector.tensor_scalar(piece[:], last_raised[u][:], decay[:, 3:4], None, op0=ALU.mult)
-            else:
-                nc.scalar.activation(piece[:], last_raised[u][:], ACT.Copy, scale=decay[:, 3:4])
-            last_weights.append(piece)
-        nc.vector.tensor_reduce(
-            result[:, :, 0:16],
-            sum_a[:].rearrange("p r (g i) -> p r g i", i=8),
-            axis=mybir.AxisListType.X,
-            op=ALU.add,
-        )
-        sums_b = [psum.tile([P, b - a, P], F32, name=f"sum_b{a}") for a, b in pieces]
+        last_weights = [keep.tile([P, b - a, P], F32, name=f"weights3_{a}") for a, b in pieces]
+        nc.vector.tensor_scalar(last_weights[0][:], last_raised[0][:], decay[:, 3:4], None, op0=ALU.mult)
+        nc.scalar.activation(last_weights[1][:], last_raised[1][:], ACT.Copy, scale=decay[:, 3:4])
+        add_up(sums_a[0], 0, 0)
+        nc.vector.tensor_scalar(last_weights[2][:], last_raised[2][:], decay[:, 3:4], None, op0=ALU.mult)
+        add_up(sums_a[1], 1, 0)
         for u, (a, b) in enumerate(pieces):
             for r in range(a, b):
-                nc.tensor.matmul(sums_b[u][:, r - a, :], weights[2][:, r, :], ident[:], start=(r == a), stop=False, is_transpose=True)
-        for u, (a, b) in enumerate(pieces):
-            sum_b = sums_b[u]
-            for r in range(a, b):
-                nc.tensor.matmul(sum_b[:, r - a, :], last_weights[u][:, r - a, :], ident[:], start=False, stop=(r == b - 1), is_transpose=True)
-            nc.vector.tensor_reduce(
-                result[:, a:b, 16:32],
-                sum_b[:].rearrange("p r (g i) -> p r g i", i=8),
-                axis=mybir.AxisListType.X,
-                op=ALU.add,
-            )
-        nc.sync.dma_start(out[0].rearrange("(s r) j -> s r j", r=4), result[:])
+                nc.tensor.matmul(
+                    sums_b[r // 2][:, r % 2, :], last_weights[u][:, r - a, :], ident[:], start=False, stop=(r % 2 == 1), is_transpose=True
+                )
+        for u in range(2):
+            add_up(sums_b[u], u, 1)
+            nc.sync.dma_start(out[0].rearrange("(s r) j -> s r j", r=4)[:, halves[u], :], results[u][:])

@@ -69,7 +69,7 @@ def tile_attend_tok_decayw_topk_kernel(tc, qT, k_words, k_scales, ls, dc, offs, 
         nc.sync.dma_start(late[:], q_rows[1][:, :, HALF:NQ])
         raw = {(0, 0): whole[:, :, 0:HALF], (1, 0): whole[:, :, HALF:NQ], (0, 1): early[:], (1, 1): late[:]}
 
-        dealt_consts = keep.tile([P, 2, 2, P], F32, name="dealt_consts")
+        dealt_consts = shared.tile([P, 2, 2, P], F32, name="dealt_consts", offset=45056)
         zero_column = keep.tile([P, 1], F32, name="zero_column")
         nc.vector.memset(zero_column[:], 0.0)
         nc.scalar.copy(dealt_consts[:].rearrange("p m h w -> p (m h w)"), zero_column[:].to_broadcast([P, NQ]))
@@ -85,8 +85,6 @@ def tile_attend_tok_decayw_topk_kernel(tc, qT, k_words, k_scales, ls, dc, offs, 
         decay = keep.tile([P, 4], F32, name="decay")
         nc.scalar.copy(decay[:], turned[:, :, 1])
 
-        listed_words = keep.tile([P, N], U32, name="listed_words", align_bytes=64)
-        nc.vector.tensor_copy(listed_words[:], key_words[:].bitcast(U32).indirect(offsets[:]))
         key_codes = {}
 
         def split(o):
@@ -99,15 +97,18 @@ def tile_attend_tok_decayw_topk_kernel(tc, qT, k_words, k_scales, ls, dc, offs, 
         scores = [psum.tile([P, N], F32, name=f"scores{c}") for c in range(4)]
 
         made = {}
-        grouped_at = {(1, 1, 0): 20480}
+        grouped_at = {(1, 1, 0): 20480, (0, 1, 0): 49152, (0, 1, 1): 50176}
+        codes_at = {(1, 0, 1): 8192, (0, 1, 0): 45056, (0, 1, 1): 45568}
 
-        def cast(h, o, m, engine):
-            if (h, o, m) in grouped_at:
+        def cast(h, o, m, engine, runs=slice(0, 16)):
+            if (h, o, m, "cast") in made:
+                grouped = made[h, o, m, "cast"]
+            elif (h, o, m) in grouped_at:
                 grouped = shared.tile([P, P, PACK], BF16, name=f"grouped{h}{o}{m}", align_bytes=64, offset=grouped_at[h, o, m])
             else:
                 grouped = keep.tile([P, P, PACK], BF16, name=f"grouped{h}{o}{m}", align_bytes=64)
-            src = raw[h, o].rearrange("p j (g m c i) -> p m g c j i", m=2, c=2, i=4)[:, m]
-            dst = grouped[:].rearrange("p (g c i) j -> p g c j i", c=2, i=4)
+            src = raw[h, o].rearrange("p j (g m c i) -> p m g c j i", m=2, c=2, i=4)[:, m, runs]
+            dst = grouped[:].rearrange("p (g c i) j -> p g c j i", c=2, i=4)[:, runs]
             if engine == "vector":
                 nc.vector.tensor_copy(dst, src)
             else:
@@ -116,8 +117,8 @@ def tile_attend_tok_decayw_topk_kernel(tc, qT, k_words, k_scales, ls, dc, offs, 
             return grouped
 
         def quantise(h, o, m, grouped):
-            if (h, o, m) == (1, 0, 1):
-                codes = shared.tile([P, P], U32, name=f"q_codes{h}{o}{m}", align_bytes=64, offset=8192)
+            if (h, o, m) in codes_at:
+                codes = shared.tile([P, P], U32, name=f"q_codes{h}{o}{m}", align_bytes=64, offset=codes_at[h, o, m])
             else:
                 codes = keep.tile([P, P], U32, name=f"q_codes{h}{o}{m}", align_bytes=64)
             plane = keep.tile([P, P], U8, name=f"q_plane{h}{o}{m}", align_bytes=64)
@@ -142,7 +143,6 @@ def tile_attend_tok_decayw_topk_kernel(tc, qT, k_words, k_scales, ls, dc, offs, 
             )
 
         first_pass = (1, 0)
-        split(1)
         rounded = [cast(0, 1, m, ("vector", "scalar")[m]) for m in range(2)]
         for m in range(2):
             quantise(0, 1, m, rounded[m])
@@ -157,34 +157,45 @@ def tile_attend_tok_decayw_topk_kernel(tc, qT, k_words, k_scales, ls, dc, offs, 
                 start=True,
                 stop=True,
             )
+        listed_words = shared.tile([P, N], U32, name="listed_words", align_bytes=64, offset=49152)
+        nc.vector.tensor_copy(listed_words[:], key_words[:].bitcast(U32).indirect(offsets[:]))
+        split(1)
         for m in range(2):
             score(0, 1, m, rounded[m])
         split(0)
-        rounded = [cast(h, 0, m, ("vector", "scalar")[m]) for h in range(2) for m in range(2)]
-        for c in range(3):
+        rounded = [cast(0, 0, 0, "vector"), cast(0, 0, 1, "scalar"), cast(1, 0, 0, "vector", slice(0, 8)), cast(1, 0, 1, "scalar")]
+        score(0, 0, 0, rounded[0])
+        cast(1, 0, 0, "vector", slice(8, 16))
+        for c in range(1, 3):
             score(c // 2, 0, c % 2, rounded[c])
-        last = [cast(1, 1, m, "vector") for m in range(2)]
+        last = [cast(1, 1, 0, "vector"), cast(1, 1, 1, "vector", slice(0, 8))]
         score(1, 1, 0, last[0])
+        cast(1, 1, 1, "vector", slice(8, 16))
         score(1, 0, 1, rounded[3])
         score(1, 1, 1, last[1])
 
         def dealt(c):
             return scores[c][:].rearrange("p (s r) -> p r s", r=4)
 
-        results = [shared.tile([P, 2, NQ // SEG], F32, name=f"result{u}", offset=(16896, 16384)[u]) for u in range(2)]
+        results = [shared.tile([P, 2, NQ // SEG], F32, name=f"result{u}", offset=(16896, 17152)[u]) for u in range(2)]
         raised = [shared.tile([P, 4, P], F32, name=f"raised{c}", offset=(0, 2048, 30720)[c]) for c in range(3)]
         weights = [shared.tile([P, 4, P], F32, name=f"weights{c}", offset=(18944, 24576, 26624)[c]) for c in range(3)]
         for c in range(2):
             nc.scalar.activation(raised[c][:], dealt(c), ACT.Exp, bias=neg_ls[:, c : c + 1])
         nc.vector.tensor_scalar(weights[0][:], raised[0][:], decay[:, 0:1], None, op0=ALU.mult)
         halves = (slice(0, 2), slice(2, 4))
+        nc.vector.tensor_scalar(weights[1][:, halves[0], :], raised[1][:, halves[0], :], decay[:, 1:2], None, op0=ALU.mult)
+        nc.vector.scalar_tensor_tensor(
+            weights[1][:, halves[1], :], raised[1][:, halves[1], :], decay[:, 1:2], weights[0][:, halves[1], :], op0=ALU.mult, op1=ALU.add
+        )
         sums_a = [psum.tile([P, 2, P], F32, name=f"sum_a{u}", tag=("sum_a", "sum_a1")[u]) for u in range(2)]
-        for u, rs in enumerate(halves):
-            nc.vector.scalar_tensor_tensor(
-                weights[1][:, rs, :], raised[1][:, rs, :], decay[:, 1:2], weights[0][:, rs, :], op0=ALU.mult, op1=ALU.add
-            )
-            for e in range(2):
-                nc.tensor.transpose(sums_a[u][:, e, :], weights[1][:, 2 * u + e, :], ident[:])
+        for u in range(2):
+            for c in range(u, 2):
+                for e in range(2):
+                    nc.tensor.matmul(
+                        sums_a[u][:, e, :], weights[c][:, 2 * u + e, :], ident[:],
+                        start=(c == u and e == 0), stop=(c == 1 and e == 1), is_transpose=True,
+                    )
 
         def add_up(sums, u, h):
             nc.vector.tensor_reduce(
@@ -207,9 +218,9 @@ def tile_attend_tok_decayw_topk_kernel(tc, qT, k_words, k_scales, ls, dc, offs, 
             last_raised.append(piece)
         last_weights = [keep.tile([P, b - a, P], F32, name=f"weights3_{a}") for a, b in pieces]
         nc.vector.tensor_scalar(last_weights[0][:], last_raised[0][:], decay[:, 3:4], None, op0=ALU.mult)
-        nc.scalar.activation(last_weights[1][:], last_raised[1][:], ACT.Copy, scale=decay[:, 3:4])
+        nc.vector.tensor_scalar(last_weights[1][:], last_raised[1][:], decay[:, 3:4], None, op0=ALU.mult)
+        nc.scalar.activation(last_weights[2][:], last_raised[2][:], ACT.Copy, scale=decay[:, 3:4])
         add_up(sums_a[0], 0, 0)
-        nc.vector.tensor_scalar(last_weights[2][:], last_raised[2][:], decay[:, 3:4], None, op0=ALU.mult)
         add_up(sums_a[1], 1, 0)
         for u, (a, b) in enumerate(pieces):
             for r in range(a, b):

@@ -100,15 +100,15 @@ def tile_attend_tok_decayw_topk_kernel(tc, qT, k_words, k_scales, ls, dc, offs, 
         grouped_at = {(1, 1, 0): 20480, (0, 1, 0): 49152, (0, 1, 1): 50176}
         codes_at = {(1, 0, 1): 8192, (0, 1, 0): 45056, (0, 1, 1): 45568}
 
-        def cast(h, o, m, engine, runs=slice(0, 16)):
+        def cast(h, o, m, engine, runs=slice(0, 16), rows=slice(0, PACK)):
             if (h, o, m, "cast") in made:
                 grouped = made[h, o, m, "cast"]
             elif (h, o, m) in grouped_at:
                 grouped = shared.tile([P, P, PACK], BF16, name=f"grouped{h}{o}{m}", align_bytes=64, offset=grouped_at[h, o, m])
             else:
                 grouped = keep.tile([P, P, PACK], BF16, name=f"grouped{h}{o}{m}", align_bytes=64)
-            src = raw[h, o].rearrange("p j (g m c i) -> p m g c j i", m=2, c=2, i=4)[:, m, runs]
-            dst = grouped[:].rearrange("p (g c i) j -> p g c j i", c=2, i=4)[:, runs]
+            src = raw[h, o].rearrange("p j (g m c i) -> p m g c j i", m=2, c=2, i=4)[:, m, runs, :, rows]
+            dst = grouped[:].rearrange("p (g c i) j -> p g c j i", c=2, i=4)[:, runs, :, rows]
             if engine == "vector":
                 nc.vector.tensor_copy(dst, src)
             else:
@@ -163,10 +163,15 @@ def tile_attend_tok_decayw_topk_kernel(tc, qT, k_words, k_scales, ls, dc, offs, 
         for m in range(2):
             score(0, 1, m, rounded[m])
         split(0)
-        rounded = [cast(0, 0, 0, "vector"), cast(0, 0, 1, "scalar"), cast(1, 0, 0, "vector", slice(0, 8)), cast(1, 0, 1, "scalar")]
-        score(0, 0, 0, rounded[0])
-        cast(1, 0, 0, "vector", slice(8, 16))
-        for c in range(1, 3):
+        for h in range(2):
+            cast(h, 0, 0, "scalar", rows=slice(0, 2))
+        rounded = [
+            cast(0, 0, 0, "vector", rows=slice(2, PACK)),
+            cast(0, 0, 1, "scalar"),
+            cast(1, 0, 0, "vector", rows=slice(2, PACK)),
+            cast(1, 0, 1, "scalar"),
+        ]
+        for c in range(3):
             score(c // 2, 0, c % 2, rounded[c])
         last = [cast(1, 1, 0, "vector"), cast(1, 1, 1, "vector", slice(0, 8))]
         score(1, 1, 0, last[0])

@@ -94,7 +94,11 @@ def tile_attend_tok_decayw_topk_kernel(tc, qT, k_words, k_scales, ls, dc, offs, 
             )
             key_codes[o] = half
 
-        scores = [psum.tile([P, N], F32, name=f"scores{c}") for c in range(4)]
+        spans = [[slice(0, HALF), slice(HALF, N)], [slice(0, N)], [slice(0, HALF), slice(HALF, N)], [slice(0, N)]]
+        scores = [
+            [psum.tile([P, span.stop - span.start], F32, name=f"scores{c}{u}", tag=f"scores{c}{u}") for u, span in enumerate(spans[c])]
+            for c in range(4)
+        ]
 
         made = {}
         grouped_at = {(1, 1, 0): 20480, (0, 1, 0): 49152, (0, 1, 1): 50176}
@@ -132,21 +136,22 @@ def tile_attend_tok_decayw_topk_kernel(tc, qT, k_words, k_scales, ls, dc, offs, 
             if (h, o, m, "plane") not in made:
                 quantise(h, o, m, grouped)
             codes, plane = made[h, o, m, "codes"], made[h, o, m, "plane"]
-            nc.tensor.matmul_mx(
-                out=scores[2 * h + m][:],
-                lhsT=codes[:].bitcast(FP8X4),
-                lhsT_scale=plane[:],
-                rhs=key_codes[o][:].bitcast(FP4X4),
-                rhs_scale=key_planes[:, o, :],
-                start=(o == first_pass[h]),
-                stop=(o != first_pass[h]),
-            )
+            for u, span in enumerate(spans[2 * h + m]):
+                nc.tensor.matmul_mx(
+                    out=scores[2 * h + m][u][:],
+                    lhsT=codes[:].bitcast(FP8X4),
+                    lhsT_scale=plane[:],
+                    rhs=key_codes[o][:, 2 * span.start : 2 * span.stop].bitcast(FP4X4),
+                    rhs_scale=key_planes[:, o, span],
+                    start=(o == first_pass[h]),
+                    stop=(o != first_pass[h]),
+                )
 
         first_pass = (1, 0)
         rounded = [cast(0, 1, m, ("vector", "scalar")[m]) for m in range(2)]
         for m in range(2):
             quantise(0, 1, m, rounded[m])
-        unread = psum.tile([P, N], F32, name="unread", tag="sum_b0")
+        unread = psum.tile([P, N], F32, name="unread", tag="sum_a1")
         for m in range(2):
             nc.tensor.matmul_mx(
                 out=unread[:],
@@ -163,13 +168,13 @@ def tile_attend_tok_decayw_topk_kernel(tc, qT, k_words, k_scales, ls, dc, offs, 
         for m in range(2):
             score(0, 1, m, rounded[m])
         split(0)
-        for h in range(2):
-            cast(h, 0, 0, "scalar", rows=slice(0, 2))
+        for h, m in ((0, 0), (1, 0), (1, 1)):
+            cast(h, 0, m, "scalar", rows=slice(0, 2))
         rounded = [
             cast(0, 0, 0, "vector", rows=slice(2, PACK)),
             cast(0, 0, 1, "scalar"),
             cast(1, 0, 0, "vector", rows=slice(2, PACK)),
-            cast(1, 0, 1, "scalar"),
+            cast(1, 0, 1, "scalar", rows=slice(2, PACK)),
         ]
         for c in range(3):
             score(c // 2, 0, c % 2, rounded[c])
@@ -179,14 +184,20 @@ def tile_attend_tok_decayw_topk_kernel(tc, qT, k_words, k_scales, ls, dc, offs, 
         score(1, 0, 1, rounded[3])
         score(1, 1, 1, last[1])
 
-        def dealt(c):
-            return scores[c][:].rearrange("p (s r) -> p r s", r=4)
+        def dealt(c, u=0):
+            return scores[c][u][:].rearrange("p (s r) -> p r s", r=4)
+
+        def raise_tile(c):
+            for u, span in enumerate(spans[c]):
+                nc.scalar.activation(
+                    raised[c][:, :, span.start // 4 : span.stop // 4], dealt(c, u), ACT.Exp, bias=neg_ls[:, c : c + 1]
+                )
 
         results = [shared.tile([P, 2, NQ // SEG], F32, name=f"result{u}", offset=(16896, 17152)[u]) for u in range(2)]
         raised = [shared.tile([P, 4, P], F32, name=f"raised{c}", offset=(0, 2048, 30720)[c]) for c in range(3)]
         weights = [shared.tile([P, 4, P], F32, name=f"weights{c}", offset=(18944, 24576, 26624)[c]) for c in range(3)]
         for c in range(2):
-            nc.scalar.activation(raised[c][:], dealt(c), ACT.Exp, bias=neg_ls[:, c : c + 1])
+            raise_tile(c)
         nc.vector.tensor_scalar(weights[0][:], raised[0][:], decay[:, 0:1], None, op0=ALU.mult)
         halves = (slice(0, 2), slice(2, 4))
         nc.vector.tensor_scalar(weights[1][:, halves[0], :], raised[1][:, halves[0], :], decay[:, 1:2], None, op0=ALU.mult)
@@ -210,9 +221,9 @@ def tile_attend_tok_decayw_topk_kernel(tc, qT, k_words, k_scales, ls, dc, offs, 
                 op=ALU.add,
             )
 
-        nc.scalar.activation(raised[2][:], dealt(2), ACT.Exp, bias=neg_ls[:, 2:3])
+        raise_tile(2)
         nc.vector.tensor_scalar(weights[2][:], raised[2][:], decay[:, 2:3], None, op0=ALU.mult)
-        sums_b = [psum.tile([P, 2, P], F32, name=f"sum_b{a}", tag=f"sum_b{a}") for a in (0, 2)]
+        sums_b = [psum.tile([P, 2, P], F32, name=f"sum_b{a}", tag=f"scores0{a // 2}") for a in (0, 2)]
         for r in range(4):
             nc.tensor.matmul(sums_b[r // 2][:, r % 2, :], weights[2][:, r, :], ident[:], start=(r % 2 == 0), stop=False, is_transpose=True)
         pieces = ((0, 2), (2, 3), (3, 4))

@@ -59,7 +59,7 @@ def tile_attend_tok_decayw_topk_kernel(tc, qT, k_words, k_scales, ls, dc, offs, 
         make_identity(nc, ident[:])
         listed_scales = keep.tile([P, N], U8, name="listed_scales", align_bytes=64)
         nc.vector.tensor_copy(listed_scales[:], scale_rows[:].indirect(offsets[:]))
-        for quad in range(4):
+        for quad in (0, 2, 1, 3):
             nc.sync.dma_start(
                 key_planes[32 * quad : 32 * quad + 4].bitcast(I32),
                 listed_scales[8 * quad : 8 * quad + 8, :].bitcast(I32),

from contextlib import ExitStack

import concourse.mybir as mybir
from concourse.masks import make_identity

F32 = mybir.dt.float32
BF16 = mybir.dt.bfloat16
I32 = mybir.dt.int32
U32 = mybir.dt.uint32
U16 = mybir.dt.uint16
U8 = mybir.dt.uint8
FP8X4 = mybir.dt.float8_e4m3fn_x4
FP4X4 = mybir.dt.float4_e2m1fn_x4
ACT = mybir.ActivationFunctionType
ALU = mybir.AluOpType

P = 128
N, T, D, NQ = 512, 2048, 1024, 512
SEG = 16
PACK = 4
PASSES = 2
HALF = 256
FLOPS = 2 * N * D * NQ


def tile_attend_tok_decayw_topk_kernel(tc, qT, k_words, k_scales, ls, dc, offs, out):
    nc = tc.nc
    with ExitStack() as ctx:
        keep = ctx.enter_context(tc.tile_pool(name="keep", bufs=1))
        shared = ctx.enter_context(tc.tile_pool(name="shared", bufs=1))
        psum = ctx.enter_context(tc.psum_pool(name="psum", bufs=1))

        q_rows = qT[0].rearrange("(o p j) w -> o p j w", o=PASSES, j=PACK)
        early = keep.tile([P, PACK, HALF], F32, name="early")
        nc.sync.dma_start(early[:, 0:1, :], q_rows[1][:, 0:1, 0:HALF])

        scale_rows = keep.tile([P, T], U8, name="scale_rows")
        nc.sync.dma_start(scale_rows[0:32, :].bitcast(I32), k_scales.rearrange("o f t -> f o t").bitcast(I32))
        nc.vector.memset(scale_rows[32:64, :].bitcast(I32), 0)
        nc.vector.memset(scale_rows[64:P, :].bitcast(I32), 0)

        offsets = keep.tile([P, N // 16], U16, name="offsets")
        nc.sync.dma_start(offsets[:], offs)

        row_consts = keep.tile([2, NQ], F32, name="row_consts")
        nc.scalar.dma_start(row_consts[0:1, :], ls[0])
        nc.scalar.dma_start(row_consts[1:2, :], dc[0])

        nc.sync.dma_start(early[:, 1:PACK, :], q_rows[1][:, 1:PACK, 0:HALF])
        key_words = shared.tile([P, T], I32, name="key_words", align_bytes=64, offset=32768)
        nc.sync.dma_start(key_words[:], k_words[0].rearrange("p t b -> p (t b)").bitcast(I32))
        whole = shared.tile([P, PACK, NQ], F32, name="whole", offset=0)
        nc.sync.dma_start(whole[:, 0:2, :], q_rows[0][:, 0:2, :])

        key_planes = keep.tile([P, PASSES, N], U8, name="key_planes", align_bytes=64)
        nc.vector.memset(key_planes[:].rearrange("p o n -> p (o n)").bitcast(I32), 0)

        ident = keep.tile([P, P], F32, name="ident")
        make_identity(nc, ident[:])
        listed_scales = keep.tile([P, N], U8, name="listed_scales", align_bytes=64)
        nc.vector.tensor_copy(listed_scales[:], scale_rows[:].indirect(offsets[:]))
        for quad in (0, 2, 1, 3):
            nc.sync.dma_start(
                key_planes[32 * quad : 32 * quad + 4].bitcast(I32),
                listed_scales[8 * quad : 8 * quad + 8, :].bitcast(I32),
            )
        nc.sync.dma_start(whole[:, 2:PACK, :], q_rows[0][:, 2:PACK, :])
        late = shared.tile([P, PACK, HALF], F32, name="late", offset=8192)
        nc.sync.dma_start(late[:], q_rows[1][:, :, HALF:NQ])
        raw = {(0, 0): whole[:, :, 0:HALF], (1, 0): whole[:, :, HALF:NQ], (0, 1): early[:], (1, 1): late[:]}

        dealt_consts = shared.tile([P, 2, 2, P], F32, name="dealt_consts", offset=45056)
        zero_column = keep.tile([P, 1], F32, name="zero_column")
        nc.vector.memset(zero_column[:], 0.0)
        nc.scalar.copy(dealt_consts[:].rearrange("p m h w -> p (m h w)"), zero_column[:].to_broadcast([P, NQ]))
        nc.scalar.copy(
            dealt_consts[0:2].rearrange("p m h (g i) -> p m (h g) i", i=8),
            row_consts[:].rearrange("p (g m i) -> p m g i", m=2, i=8),
        )
        turned = psum.tile([P, 4, P], F32, name="turned", tag="sum_a")
        for c in range(4):
            nc.tensor.transpose(turned[:, c, :], dealt_consts[:, c % 2, c // 2, :], ident[:])
        neg_ls = shared.tile([P, 4], F32, name="neg_ls", offset=16384)
        nc.scalar.activation(neg_ls[:], turned[:, :, 0], ACT.Copy, scale=-1.0)
        decay = keep.tile([P, 4], F32, name="decay")
        nc.scalar.copy(decay[:], turned[:, :, 1])

        key_codes = {}

        def split(o):
            half = keep.tile([P, 2 * N], U8, name=f"key_codes{o}", align_bytes=64)
            nc.vector.tensor_copy(
                half[:].bitcast(U16), listed_words[:].bitcast(U16).rearrange("p (n o) -> p o n", o=PASSES)[:, o, :]
            )
            key_codes[o] = half

        spans = [[slice(0, HALF), slice(HALF, N)], [slice(0, N)], [slice(0, HALF), slice(HALF, N)], [slice(0, N)]]
        scores = [
            [psum.tile([P, span.stop - span.start], F32, name=f"scores{c}{u}", tag=f"scores{c}{u}") for u, span in enumerate(spans[c])]
            for c in range(4)
        ]

        made = {}
        grouped_at = {(1, 1, 0): 20480, (0, 1, 0): 49152, (0, 1, 1): 50176}
        codes_at = {(1, 0, 1): 8192, (0, 1, 0): 45056, (0, 1, 1): 45568}

        def cast(h, o, m, engine, runs=slice(0, 16), rows=slice(0, PACK)):
            if (h, o, m, "cast") in made:
                grouped = made[h, o, m, "cast"]
            elif (h, o, m) in grouped_at:
                grouped = shared.tile([P, P, PACK], BF16, name=f"grouped{h}{o}{m}", align_bytes=64, offset=grouped_at[h, o, m])
            else:
                grouped = keep.tile([P, P, PACK], BF16, name=f"grouped{h}{o}{m}", align_bytes=64)
            src = raw[h, o].rearrange("p j (g m c i) -> p m g c j i", m=2, c=2, i=4)[:, m, runs, :, rows]
            dst = grouped[:].rearrange("p (g c i) j -> p g c j i", c=2, i=4)[:, runs, :, rows]
            if engine == "vector":
                nc.vector.tensor_copy(dst, src)
            else:
                nc.scalar.copy(dst, src)
            made[h, o, m, "cast"] = grouped
            return grouped

        def quantise(h, o, m, grouped):
            if (h, o, m) in codes_at:
                codes = shared.tile([P, P], U32, name=f"q_codes{h}{o}{m}", align_bytes=64, offset=codes_at[h, o, m])
            else:
                codes = keep.tile([P, P], U32, name=f"q_codes{h}{o}{m}", align_bytes=64)
            plane = keep.tile([P, P], U8, name=f"q_plane{h}{o}{m}", align_bytes=64)
            made[h, o, m, "codes"] = codes
            nc.vector.quantize_mx(
                out=codes[:].bitcast(FP8X4), scales=plane[:], in_=grouped[:].rearrange("p w j -> p (w j)")
            )
            made[h, o, m, "plane"] = plane

        def score(h, o, m, grouped):
            if (h, o, m, "plane") not in made:
                quantise(h, o, m, grouped)
            codes, plane = made[h, o, m, "codes"], made[h, o, m, "plane"]
            for u, span in enumerate(spans[2 * h + m]):
                nc.tensor.matmul_mx(
                    out=scores[2 * h + m][u][:],
                    lhsT=codes[:].bitcast(FP8X4),
                    lhsT_scale=plane[:],
                    rhs=key_codes[o][:, 2 * span.start : 2 * span.stop].bitcast(FP4X4),
                    rhs_scale=key_planes[:, o, span],
                    start=(o == first_pass[h]),
                    stop=(o != first_pass[h]),
                )

        first_pass = (1, 0)
        rounded = [cast(0, 1, m, ("vector", "scalar")[m]) for m in range(2)]
        for m in range(2):
            quantise(0, 1, m, rounded[m])
        unread = psum.tile([P, N], F32, name="unread", tag="sum_a1")
        for m in range(2):
            nc.tensor.matmul_mx(
                out=unread[:],
                lhsT=made[0, 1, m, "codes"][:].bitcast(FP8X4),
                lhsT_scale=made[0, 1, m, "plane"][:],
                rhs=key_words[:, 0:HALF].bitcast(U8).bitcast(FP4X4),
                rhs_scale=listed_scales[:],
                start=True,
                stop=True,
            )
        listed_words = shared.tile([P, N], U32, name="listed_words", align_bytes=64, offset=49152)
        nc.vector.tensor_copy(listed_words[:], key_words[:].bitcast(U32).indirect(offsets[:]))
        split(1)
        for m in range(2):
            score(0, 1, m, rounded[m])
        split(0)
        for h, m in ((0, 0), (1, 0), (1, 1)):
            cast(h, 0, m, "scalar", rows=slice(0, 2))
        rounded = [
            cast(0, 0, 0, "vector", rows=slice(2, PACK)),
            cast(0, 0, 1, "scalar"),
            cast(1, 0, 0, "vector", rows=slice(2, PACK)),
            cast(1, 0, 1, "scalar", rows=slice(2, PACK)),
        ]
        for c in range(3):
            score(c // 2, 0, c % 2, rounded[c])
        last = [cast(1, 1, 0, "vector"), cast(1, 1, 1, "vector", slice(0, 8))]
        score(1, 1, 0, last[0])
        cast(1, 1, 1, "vector", slice(8, 16))
        score(1, 0, 1, rounded[3])
        score(1, 1, 1, last[1])

        def dealt(c, u=0):
            return scores[c][u][:].rearrange("p (s r) -> p r s", r=4)

        def raise_tile(c):
            for u, span in enumerate(spans[c]):
                nc.scalar.activation(
                    raised[c][:, :, span.start // 4 : span.stop // 4], dealt(c, u), ACT.Exp, bias=neg_ls[:, c : c + 1]
                )

        results = [shared.tile([P, 2, NQ // SEG], F32, name=f"result{u}", offset=(16896, 17152)[u]) for u in range(2)]
        raised = [shared.tile([P, 4, P], F32, name=f"raised{c}", offset=(0, 2048, 30720)[c]) for c in range(3)]
        weights = [shared.tile([P, 4, P], F32, name=f"weights{c}", offset=(18944, 24576, 26624)[c]) for c in range(3)]
        for c in range(2):
            raise_tile(c)
        nc.vector.tensor_scalar(weights[0][:], raised[0][:], decay[:, 0:1], None, op0=ALU.mult)
        halves = (slice(0, 2), slice(2, 4))
        nc.vector.tensor_scalar(weights[1][:, halves[0], :], raised[1][:, halves[0], :], decay[:, 1:2], None, op0=ALU.mult)
        nc.vector.scalar_tensor_tensor(
            weights[1][:, halves[1], :], raised[1][:, halves[1], :], decay[:, 1:2], weights[0][:, halves[1], :], op0=ALU.mult, op1=ALU.add
        )
        sums_a = [psum.tile([P, 2, P], F32, name=f"sum_a{u}", tag=("sum_a", "sum_a1")[u]) for u in range(2)]
        for u in range(2):
            for c in range(u, 2):
                for e in range(2):
                    nc.tensor.matmul(
                        sums_a[u][:, e, :], weights[c][:, 2 * u + e, :], ident[:],
                        start=(c == u and e == 0), stop=(c == 1 and e == 1), is_transpose=True,
                    )

        def add_up(sums, u, h):
            nc.vector.tensor_reduce(
                results[u][:, :, 16 * h : 16 * h + 16],
                sums[:].rearrange("p r (g i) -> p r g i", i=8),
                axis=mybir.AxisListType.X,
                op=ALU.add,
            )

        raise_tile(2)
        nc.vector.tensor_scalar(weights[2][:], raised[2][:], decay[:, 2:3], None, op0=ALU.mult)
        sums_b = [psum.tile([P, 2, P], F32, name=f"sum_b{a}", tag=f"scores0{a // 2}") for a in (0, 2)]
        for r in range(4):
            nc.tensor.matmul(sums_b[r // 2][:, r % 2, :], weights[2][:, r, :], ident[:], start=(r % 2 == 0), stop=False, is_transpose=True)
        pieces = ((0, 2), (2, 3), (3, 4))
        last_raised = []
        for a, b in pieces:
            piece = keep.tile([P, b - a, P], F32, name=f"raised3_{a}")
            nc.scalar.activation(piece[:], dealt(3)[:, a:b, :], ACT.Exp, bias=neg_ls[:, 3:4])
            last_raised.append(piece)
        last_weights = [keep.tile([P, b - a, P], F32, name=f"weights3_{a}") for a, b in pieces]
        nc.vector.tensor_scalar(last_weights[0][:], last_raised[0][:], decay[:, 3:4], None, op0=ALU.mult)
        nc.vector.tensor_scalar(last_weights[1][:], last_raised[1][:], decay[:, 3:4], None, op0=ALU.mult)
        nc.scalar.activation(last_weights[2][:], last_raised[2][:], ACT.Copy, scale=decay[:, 3:4])
        add_up(sums_a[0], 0, 0)
        add_up(sums_a[1], 1, 0)
        for u, (a, b) in enumerate(pieces):
            for r in range(a, b):
                nc.tensor.matmul(
                    sums_b[r // 2][:, r % 2, :], last_weights[u][:, r - a, :], ident[:], start=False, stop=(r % 2 == 1), is_transpose=True
                )
        for u in range(2):
            add_up(sums_b[u], u, 1)
            nc.sync.dma_start(out[0].rearrange("(s r) j -> s r j", r=4)[:, halves[u], :], results[u][:])
